import numpy as np
import ml_dtypes


def mxq(x, axis, fmt="e4m3"):
    dtype, down = {"e4m3": (ml_dtypes.float8_e4m3fn, 7), "e5m2": (ml_dtypes.float8_e5m2, 14)}[fmt]
    v = np.moveaxis(np.asarray(x, np.float32).astype(ml_dtypes.bfloat16).astype(np.float64), axis, -1)
    blocks = v.reshape(v.shape[:-1] + (-1, 32))
    amax = np.abs(blocks).max(-1, keepdims=True)
    byte = np.maximum(np.where(amax > 0, np.frexp(amax)[1] - 1 + 127, 0) - down, 1)
    scale = np.exp2(byte - 127.0)
    codes = (blocks / scale).astype(np.float32).astype(dtype).astype(np.float64)
    return np.moveaxis((codes * scale).reshape(v.shape), -1, axis)


WIDE = False


def mx_kscale(k):
    if not WIDE:
        return np.ones(k)
    levels = np.array([10, -10, 5, -5, 0])
    if k % 512:
        return np.exp2(np.random.permutation(np.resize(levels, k // 32))).repeat(32)
    a = np.empty((k // 512, 16))
    for p in range(k // 512):
        a[p, :8] = np.random.permutation(np.resize(levels, 8))
        for g in range(8):
            far = levels[np.abs(levels - a[p, g]) >= 10]
            a[p, g + 8] = far[np.random.randint(len(far))]
    return np.exp2(a.ravel()).repeat(32)


def f64(x):
    return np.asarray(x).astype(np.float64)


def striped(idx):
    return np.tile(idx.reshape(-1, 16).T, (8, 1)).astype(np.uint16)


def unstriped(offs):
    return offs[:16].T.reshape(-1).astype(np.int64)


def pack_weight(w):
    k, n = w.shape
    w = f64(np.asarray(w, np.float32).astype(ml_dtypes.bfloat16)).reshape(k // 32, 32, n)
    amax = np.abs(w).max(1)
    byte = np.clip(np.where(amax > 0, np.frexp(amax)[1] - 1 + 127 - 7, 1), 1, 254)
    scaled = (w * np.exp2(127.0 - byte)[:, None, :]).reshape(k, n).astype(np.float32)
    words = np.ascontiguousarray(scaled.reshape(k // 512, 128, 4, n).transpose(0, 1, 3, 2)).astype(ml_dtypes.float8_e4m3fn).view(np.uint8)
    return words, np.ascontiguousarray(byte.astype(np.uint8).reshape(k // 512, 16, n))


def unpack_weight(words, scales):
    g, p, n, _ = words.shape
    vals = np.ascontiguousarray(words).view(ml_dtypes.float8_e4m3fn).astype(np.float64) * np.repeat(np.exp2(scales.astype(np.float64) - 127.0), 8, axis=1)[..., None]
    return vals.transpose(0, 1, 3, 2).reshape(g * 512, n)


K, T, S, N, U = 512, 4096, 1024, 256, 2048
P = 2 ** 7


def setup_inputs():
    n = np.random.standard_normal
    s = mx_kscale(K)[:, None]
    packed_xT = pack_weight(n((K, T)) * s)
    return {
        "x_words": packed_xT[0],
        "x_scales": packed_xT[1],
        "mem": n((N, U)).astype(np.float32),
        "w1": (n((K, N)) / np.sqrt(K) / s).astype(np.float32),
        "old": np.tile(np.random.uniform(0.5, 0.95, S), (P, 1)).astype(np.float32),
        "new": np.tile(np.random.uniform(0.05, 0.5, S), (P, 1)).astype(np.float32),
        "offs": striped(np.random.permutation(T)[:S]),
        "slot": striped(np.random.permutation(U)[:S]),
    }


def reference(x_words, x_scales, mem, w1, old, new, offs, slot):
    xq = unpack_weight(x_words, x_scales)[:, unstriped(offs)]
    y = mxq(f64(w1), 0, "e4m3").T @ xq
    out = f64(mem).copy()
    out[:, unstriped(slot)] = f64(mem)[:, unstriped(slot)] * f64(old)[:1] + y * f64(new)[:1]
    return out

@@ -1,0 +1,136 @@
+from contextlib import ExitStack
+
+import concourse.mybir as mybir
+from concourse.masks import make_identity
+
+K, T, S, N, U = 512, 4096, 1024, 256, 2048
+FLOPS = 2 * K * N * S
+
+F32 = mybir.dt.float32
+BF16 = mybir.dt.bfloat16
+I32 = mybir.dt.int32
+U32 = mybir.dt.uint32
+U16 = mybir.dt.uint16
+U8 = mybir.dt.uint8
+FP8X4 = mybir.dt.float8_e4m3fn_x4
+COPY = mybir.ActivationFunctionType.Copy
+
+P = 128
+PACK = 4
+STRIPE = 16
+HALF = 512
+CHUNKS = S // P
+PER_HALF = HALF // P
+ROW_BLOCKS = N // P
+
+
+def tile_picked_ema_none_p_kernel(
+    tc, x_words, x_scales, mem, w1, old, new, offs, slot, out
+):
+    nc = tc.nc
+    with ExitStack() as ctx:
+        keep = ctx.enter_context(tc.tile_pool(name="keep", bufs=1))
+        psum = ctx.enter_context(tc.psum_pool(name="psum", bufs=1))
+
+        offs_sb = keep.tile([P, S // STRIPE], U16, name="offs_sb")
+        slot_sb = keep.tile([P, S // STRIPE], U16, name="slot_sb")
+        words = keep.tile([P, T], U32, name="words")
+        scales = keep.tile([P, T], U8, name="scales")
+        memory = [keep.tile([P, U], F32, name=f"memory{b}") for b in range(ROW_BLOCKS)]
+        w_raw = keep.tile([P, PACK, N], F32, name="w_raw")
+        factor_rows = keep.tile([P, P], F32, name="factor_rows")
+        identity = keep.tile([P, P], F32, name="identity")
+
+        nc.vector.memset(scales[:].bitcast(I32), 0)
+        make_identity(nc, identity[:])
+
+        nc.sync.dma_start(slot_sb[:], slot)
+        nc.sync.dma_start(offs_sb[:], offs)
+        nc.sync.dma_start(factor_rows[0:64, :], old[0:8, :].rearrange("r (c i) -> (r c) i", i=P))
+        nc.sync.dma_start(factor_rows[64:128, :], new[0:8, :].rearrange("r (c i) -> (r c) i", i=P))
+        nc.sync.dma_start(memory[0][:], mem[0:P, :])
+        for q in range(4):
+            nc.sync.dma_start(scales[32 * q : 32 * q + 4, :].bitcast(I32), x_scales[0, 4 * q : 4 * q + 4, :].bitcast(I32))
+        nc.sync.dma_start(w_raw[:], w1.rearrange("(p j) n -> p j n", j=PACK))
+        nc.sync.dma_start(words[:].bitcast(I32), x_words[0].rearrange("p n t -> p (n t)").bitcast(I32))
+        nc.sync.dma_start(memory[1][:], mem[P : 2 * P, :])
+
+        halves = range(S // HALF)
+        mixing = [psum.tile([P, HALF], F32, name=f"mixing{h}") for h in halves]
+        product = psum.tile([P, HALF], F32, name="product")
+
+        factors = keep.tile([P, P], F32, name="factors")
+        nc.tensor.transpose(product[:, 0:P], factor_rows[:], identity[:])
+        nc.scalar.copy(factors[:], product[:, 0:P])
+
+        picked = [keep.tile([P, S], F32, name=f"picked{b}") for b in range(ROW_BLOCKS)]
+        kept = keep.tile([P, S], F32, name="kept")
+        fresh = keep.tile([P, S], F32, name="fresh")
+        x_codes = [keep.tile([P, HALF], U32, name=f"x_codes{h}", align_bytes=64) for h in halves]
+        x_scale = keep.tile([P, S], U8, name="x_scale", align_bytes=64)
+        w_grouped = keep.tile([P, N, PACK], BF16, name="w_grouped", align_bytes=64)
+        w_codes = keep.tile([P, N], U32, name="w_codes", align_bytes=64)
+        w_scale = keep.tile([P, N], U8, name="w_scale", align_bytes=64)
+
+        def cols(i):
+            return slice(i * P, (i + 1) * P)
+
+        def list_half(offsets, h):
+            return offsets[:, h * HALF // STRIPE : (h + 1) * HALF // STRIPE]
+
+        def gather_memory(b):
+            nc.vector.tensor_copy(picked[b][:], memory[b][:].indirect(slot_sb[:]))
+
+        def scale_memory(b, h):
+            for c in range(PER_HALF):
+                nc.tensor.transpose(mixing[h][:, cols(c)], picked[b][:, cols(h * PER_HALF + c)], identity[:])
+            for c in range(PER_HALF):
+                chunk = h * PER_HALF + c
+                nc.scalar.activation(kept[:, cols(chunk)], mixing[h][:, cols(c)], COPY, scale=factors[:, chunk : chunk + 1])
+
+        def project(b, h):
+            for c in range(PER_HALF):
+                nc.tensor.matmul_mx(
+                    out=product[:, cols(c)],
+                    lhsT=x_codes[h][:, cols(c)].bitcast(FP8X4),
+                    lhsT_scale=x_scale[:, cols(h * PER_HALF + c)],
+                    rhs=w_codes[:, cols(b)].bitcast(FP8X4),
+                    rhs_scale=w_scale[:, cols(b)],
+                    start=True,
+                    stop=True,
+                )
+            for c in range(PER_HALF):
+                chunk = h * PER_HALF + c
+                nc.scalar.activation(fresh[:, cols(chunk)], product[:, cols(c)], COPY, scale=factors[:, 64 + chunk : 64 + chunk + 1])
+
+        def blend(h, target):
+            for c in range(PER_HALF):
+                chunk = h * PER_HALF + c
+                nc.tensor.matmul(mixing[h][:, cols(c)], kept[:, cols(chunk)], identity[:], start=True, stop=False, is_transpose=True)
+                nc.tensor.matmul(mixing[h][:, cols(c)], fresh[:, cols(chunk)], identity[:], start=False, stop=True, is_transpose=True)
+            nc.scalar.copy(target, mixing[h][:])
+
+        gather_memory(0)
+        nc.vector.tensor_copy(x_scale[:], scales[:].indirect(offs_sb[:]))
+        nc.scalar.copy(w_grouped[:], w_raw[:].rearrange("p j n -> p n j"))
+        nc.vector.quantize_mx(out=w_codes[:].bitcast(FP8X4), scales=w_scale[:], in_=w_grouped[:].rearrange("p n j -> p (n j)"))
+        for h in halves:
+            scale_memory(0, h)
+        for h in halves:
+            nc.vector.tensor_copy(x_codes[h][:], words[:].indirect(list_half(offs_sb, h)))
+        gather_memory(1)
+
+        for h in halves:
+            blended = keep.tile([P, HALF], F32, name=f"blended0_{h}")
+            project(0, h)
+            blend(h, blended[:])
+            nc.vector.tensor_copy(memory[0][:].indirect(list_half(slot_sb, h)), blended[:])
+        nc.sync.dma_start(out[0:P, :], memory[0][:])
+
+        blended = keep.tile([P, S], F32, name="blended1")
+        for h in halves:
+            project(1, h)
+            scale_memory(1, h)
+            blend(h, blended[:, h * HALF : (h + 1) * HALF])
+        nc.vector.tensor_copy(memory[1][:].indirect(slot_sb[:]), blended[:])
+        nc.sync.dma_start(out[P : 2 * P, :], memory[1][:])

@@ -35,7 +35,7 @@ def tile_picked_ema_none_p_kernel(
         offs_sb = keep.tile([P, S // STRIPE], U16, name="offs_sb")
         slot_sb = keep.tile([P, S // STRIPE], U16, name="slot_sb")
         words = keep.tile([P, T], U32, name="words")
-        scales = keep.tile([P, T], U8, name="scales")
+        scales = keep.tile([P, T], U8, name="scales", tag="early")
         memory = [keep.tile([P, U], F32, name=f"memory{b}") for b in range(ROW_BLOCKS)]
         w_raw = keep.tile([P, PACK, N], F32, name="w_raw")
         factor_rows = keep.tile([P, P], F32, name="factor_rows")
@@ -44,14 +44,13 @@ def tile_picked_ema_none_p_kernel(
         nc.vector.memset(scales[:].bitcast(I32), 0)
         make_identity(nc, identity[:])
 
-        nc.sync.dma_start(slot_sb[:], slot)
+        nc.sync.dma_start(w_raw[:], w1.rearrange("(p j) n -> p j n", j=PACK))
         nc.sync.dma_start(offs_sb[:], offs)
+        nc.sync.dma_start(slot_sb[:], slot)
         nc.sync.dma_start(factor_rows[0:64, :], old[0:8, :].rearrange("r (c i) -> (r c) i", i=P))
         nc.sync.dma_start(factor_rows[64:128, :], new[0:8, :].rearrange("r (c i) -> (r c) i", i=P))
+        nc.sync.dma_start(scales[0:P:8, :].bitcast(I32), x_scales[0].bitcast(I32))
         nc.sync.dma_start(memory[0][:], mem[0:P, :])
-        for q in range(4):
-            nc.sync.dma_start(scales[32 * q : 32 * q + 4, :].bitcast(I32), x_scales[0, 4 * q : 4 * q + 4, :].bitcast(I32))
-        nc.sync.dma_start(w_raw[:], w1.rearrange("(p j) n -> p j n", j=PACK))
         nc.sync.dma_start(words[:].bitcast(I32), x_words[0].rearrange("p n t -> p (n t)").bitcast(I32))
         nc.sync.dma_start(memory[1][:], mem[P : 2 * P, :])
 
@@ -63,11 +62,16 @@ def tile_picked_ema_none_p_kernel(
         nc.tensor.transpose(product[:, 0:P], factor_rows[:], identity[:])
         nc.scalar.copy(factors[:], product[:, 0:P])
 
-        picked = [keep.tile([P, S], F32, name=f"picked{b}") for b in range(ROW_BLOCKS)]
+        spread_scale = keep.tile([P, S], U8, name="spread_scale")
+        x_scale = keep.tile([P, S], U8, name="x_scale", align_bytes=64)
+        nc.vector.memset(x_scale[:].bitcast(I32), 0)
+        nc.vector.tensor_copy(spread_scale[:], scales[:].indirect(offs_sb[:]))
+        for r in range(4):
+            nc.scalar.dma_start(x_scale[r:P:32, :].bitcast(I32), spread_scale[8 * r : P : 32, :].bitcast(I32))
+        picked = [keep.tile([P, S], F32, name="picked0", tag="early"), keep.tile([P, S], F32, name="picked1")]
         kept = keep.tile([P, S], F32, name="kept")
         fresh = keep.tile([P, S], F32, name="fresh")
         x_codes = [keep.tile([P, HALF], U32, name=f"x_codes{h}", align_bytes=64) for h in halves]
-        x_scale = keep.tile([P, S], U8, name="x_scale", align_bytes=64)
         w_grouped = keep.tile([P, N, PACK], BF16, name="w_grouped", align_bytes=64)
         w_codes = keep.tile([P, N], U32, name="w_codes", align_bytes=64)
         w_scale = keep.tile([P, N], U8, name="w_scale", align_bytes=64)
@@ -111,7 +115,6 @@ def tile_picked_ema_none_p_kernel(
             nc.scalar.copy(target, mixing[h][:])
 
         gather_memory(0)
-        nc.vector.tensor_copy(x_scale[:], scales[:].indirect(offs_sb[:]))
         nc.scalar.copy(w_grouped[:], w_raw[:].rearrange("p j n -> p n j"))
         nc.vector.quantize_mx(out=w_codes[:].bitcast(FP8X4), scales=w_scale[:], in_=w_grouped[:].rearrange("p n j -> p (n j)"))
         for h in halves:

@@ -35,13 +35,14 @@ def tile_picked_ema_none_p_kernel(
         offs_sb = keep.tile([P, S // STRIPE], U16, name="offs_sb")
         slot_sb = keep.tile([P, S // STRIPE], U16, name="slot_sb")
         words = keep.tile([P, T], U32, name="words")
-        scales = keep.tile([P, T], U8, name="scales", tag="early")
+        scales = keep.tile([P, T], U8, name="scales")
         memory = [keep.tile([P, U], F32, name=f"memory{b}") for b in range(ROW_BLOCKS)]
         w_raw = keep.tile([P, PACK, N], F32, name="w_raw")
         factor_rows = keep.tile([P, P], F32, name="factor_rows")
         identity = keep.tile([P, P], F32, name="identity")
 
-        nc.vector.memset(scales[:].bitcast(I32), 0)
+        nc.vector.memset(scales[:, 0 : T // 2].bitcast(I32), 0)
+        nc.gpsimd.memset(scales[:, T // 2 : T].bitcast(I32), 0)
         make_identity(nc, identity[:])
 
         nc.sync.dma_start(w_raw[:], w1.rearrange("(p j) n -> p j n", j=PACK))
@@ -56,11 +57,12 @@ def tile_picked_ema_none_p_kernel(
 
         halves = range(S // HALF)
         mixing = [psum.tile([P, HALF], F32, name=f"mixing{h}") for h in halves]
-        product = psum.tile([P, HALF], F32, name="product")
+        totals = [psum.tile([P, HALF], F32, name=f"total{h}") for h in halves]
+        product = [psum.tile([P, HALF], F32, name=f"product{i}") for i in range(2)]
 
         factors = keep.tile([P, P], F32, name="factors")
-        nc.tensor.transpose(product[:, 0:P], factor_rows[:], identity[:])
-        nc.scalar.copy(factors[:], product[:, 0:P])
+        nc.tensor.transpose(totals[0][:, 0:P], factor_rows[:], identity[:])
+        nc.scalar.copy(factors[:], totals[0][:, 0:P])
 
         spread_scale = keep.tile([P, S], U8, name="spread_scale")
         x_scale = keep.tile([P, S], U8, name="x_scale", align_bytes=64)
@@ -68,8 +70,8 @@ def tile_picked_ema_none_p_kernel(
         nc.vector.tensor_copy(spread_scale[:], scales[:].indirect(offs_sb[:]))
         for r in range(4):
             nc.scalar.dma_start(x_scale[r:P:32, :].bitcast(I32), spread_scale[8 * r : P : 32, :].bitcast(I32))
-        picked = [keep.tile([P, S], F32, name="picked0", tag="early"), keep.tile([P, S], F32, name="picked1")]
-        kept = keep.tile([P, S], F32, name="kept")
+        picked = [[keep.tile([P, HALF], F32, name=f"picked{b}_{h}") for h in halves] for b in range(ROW_BLOCKS)]
+        kept = [keep.tile([P, S], F32, name=f"kept{b}") for b in range(ROW_BLOCKS)]
         fresh = keep.tile([P, S], F32, name="fresh")
         x_codes = [keep.tile([P, HALF], U32, name=f"x_codes{h}", align_bytes=64) for h in halves]
         w_grouped = keep.tile([P, N, PACK], BF16, name="w_grouped", align_bytes=64)
@@ -83,19 +85,20 @@ def tile_picked_ema_none_p_kernel(
             return offsets[:, h * HALF // STRIPE : (h + 1) * HALF // STRIPE]
 
         def gather_memory(b):
-            nc.vector.tensor_copy(picked[b][:], memory[b][:].indirect(slot_sb[:]))
+            for h in halves:
+                nc.vector.tensor_copy(picked[b][h][:], memory[b][:].indirect(list_half(slot_sb, h)))
 
         def scale_memory(b, h):
             for c in range(PER_HALF):
-                nc.tensor.transpose(mixing[h][:, cols(c)], picked[b][:, cols(h * PER_HALF + c)], identity[:])
+                nc.tensor.transpose(mixing[h][:, cols(c)], picked[b][h][:, cols(c)], identity[:])
             for c in range(PER_HALF):
                 chunk = h * PER_HALF + c
-                nc.scalar.activation(kept[:, cols(chunk)], mixing[h][:, cols(c)], COPY, scale=factors[:, chunk : chunk + 1])
+                nc.scalar.activation(kept[b][:, cols(chunk)], mixing[h][:, cols(c)], COPY, scale=factors[:, chunk : chunk + 1])
 
-        def project(b, h):
-            for c in range(PER_HALF):
+        def project(b, h, bank, members):
+            for c in members:
                 nc.tensor.matmul_mx(
-                    out=product[:, cols(c)],
+                    out=bank[:, cols(c)],
                     lhsT=x_codes[h][:, cols(c)].bitcast(FP8X4),
                     lhsT_scale=x_scale[:, cols(h * PER_HALF + c)],
                     rhs=w_codes[:, cols(b)].bitcast(FP8X4),
@@ -103,37 +106,50 @@ def tile_picked_ema_none_p_kernel(
                     start=True,
                     stop=True,
                 )
-            for c in range(PER_HALF):
+            for c in members:
                 chunk = h * PER_HALF + c
-                nc.scalar.activation(fresh[:, cols(chunk)], product[:, cols(c)], COPY, scale=factors[:, 64 + chunk : 64 + chunk + 1])
+                nc.scalar.activation(fresh[:, cols(chunk)], bank[:, cols(c)], COPY, scale=factors[:, 64 + chunk : 64 + chunk + 1])
 
-        def blend(h, target):
+        def turn_back(bank, terms, opens):
             for c in range(PER_HALF):
-                chunk = h * PER_HALF + c
-                nc.tensor.matmul(mixing[h][:, cols(c)], kept[:, cols(chunk)], identity[:], start=True, stop=False, is_transpose=True)
-                nc.tensor.matmul(mixing[h][:, cols(c)], fresh[:, cols(chunk)], identity[:], start=False, stop=True, is_transpose=True)
-            nc.scalar.copy(target, mixing[h][:])
+                nc.tensor.matmul(
+                    bank[:, cols(c)], terms[c], identity[:], start=opens and c == 0, stop=not opens and c == PER_HALF - 1, is_transpose=True
+                )
+
+        def kept_terms(b, h):
+            return [kept[b][:, cols(h * PER_HALF + c)] for c in range(PER_HALF)]
+
+        def fresh_terms(h):
+            return [fresh[:, cols(h * PER_HALF + c)] for c in range(PER_HALF)]
+
+        def scatter(b, h, bank):
+            blended = keep.tile([P, HALF], F32, name=f"blended{b}_{h}")
+            nc.scalar.copy(blended[:], bank[:])
+            nc.vector.tensor_copy(memory[b][:].indirect(list_half(slot_sb, h)), blended[:])
 
         gather_memory(0)
         nc.scalar.copy(w_grouped[:], w_raw[:].rearrange("p j n -> p n j"))
         nc.vector.quantize_mx(out=w_codes[:].bitcast(FP8X4), scales=w_scale[:], in_=w_grouped[:].rearrange("p n j -> p (n j)"))
         for h in halves:
             scale_memory(0, h)
+            turn_back(mixing[h], kept_terms(0, h), opens=True)
         for h in halves:
             nc.vector.tensor_copy(x_codes[h][:], words[:].indirect(list_half(offs_sb, h)))
         gather_memory(1)
 
-        for h in halves:
-            blended = keep.tile([P, HALF], F32, name=f"blended0_{h}")
-            project(0, h)
-            blend(h, blended[:])
-            nc.vector.tensor_copy(memory[0][:].indirect(list_half(slot_sb, h)), blended[:])
+        project(0, 0, product[0], range(0, 2))
+        project(0, 0, product[1], range(2, 4))
+        turn_back(mixing[0], fresh_terms(0), opens=False)
+        scatter(0, 0, mixing[0])
+        project(0, 1, product[1], range(PER_HALF))
+        turn_back(mixing[1], fresh_terms(1), opens=False)
+        scatter(0, 1, mixing[1])
         nc.sync.dma_start(out[0:P, :], memory[0][:])
 
-        blended = keep.tile([P, S], F32, name="blended1")
         for h in halves:
-            project(1, h)
+            project(1, h, product[1], range(PER_HALF))
+            turn_back(totals[h], fresh_terms(h), opens=True)
             scale_memory(1, h)
-            blend(h, blended[:, h * HALF : (h + 1) * HALF])
-        nc.vector.tensor_copy(memory[1][:].indirect(slot_sb[:]), blended[:])
+            turn_back(totals[h], kept_terms(1, h), opens=False)
+            scatter(1, h, totals[h])
         nc.sync.dma_start(out[P : 2 * P, :], memory[1][:])

@@ -35,7 +35,7 @@ def tile_picked_ema_none_p_kernel(
         offs_sb = keep.tile([P, S // STRIPE], U16, name="offs_sb")
         slot_sb = keep.tile([P, S // STRIPE], U16, name="slot_sb")
         words = keep.tile([P, T], U32, name="words")
-        scales = keep.tile([P, T], U8, name="scales")
+        scales = keep.tile([P, T], U8, name="scales", tag="scales_then_w_codes", align_bytes=64)
         memory = [keep.tile([P, U], F32, name=f"memory{b}") for b in range(ROW_BLOCKS)]
         w_raw = keep.tile([P, PACK, N], F32, name="w_raw")
         factor_rows = keep.tile([P, P], F32, name="factor_rows")
@@ -75,7 +75,7 @@ def tile_picked_ema_none_p_kernel(
         fresh = keep.tile([P, S], F32, name="fresh")
         x_codes = [keep.tile([P, HALF], U32, name=f"x_codes{h}", align_bytes=64) for h in halves]
         w_grouped = keep.tile([P, N, PACK], BF16, name="w_grouped", align_bytes=64)
-        w_codes = keep.tile([P, N], U32, name="w_codes", align_bytes=64)
+        w_codes = keep.tile([P, N], U32, name="w_codes", tag="scales_then_w_codes", align_bytes=64)
         w_scale = keep.tile([P, N], U8, name="w_scale", align_bytes=64)
 
         def cols(i):

@@ -40,43 +40,47 @@ def tile_picked_ema_none_p_kernel(
         w_raw = keep.tile([P, PACK, N], F32, name="w_raw")
         factor_rows = keep.tile([P, P], F32, name="factor_rows")
         identity = keep.tile([P, P], F32, name="identity")
+        x_scale = keep.tile([P, S], U8, name="x_scale", align_bytes=64)
 
-        nc.vector.memset(scales[:, 0 : T // 2].bitcast(I32), 0)
-        nc.gpsimd.memset(scales[:, T // 2 : T].bitcast(I32), 0)
+        OLD_ROW = P - 2 * CHUNKS
+        NEW_ROW = P - CHUNKS
+        nc.vector.memset(scales[:].bitcast(I32), 0)
+        nc.vector.memset(x_scale[:].bitcast(I32), 0)
+        nc.vector.memset(factor_rows[0:OLD_ROW, :], 0.0)
         make_identity(nc, identity[:])
 
         nc.sync.dma_start(w_raw[:], w1.rearrange("(p j) n -> p j n", j=PACK))
         nc.sync.dma_start(offs_sb[:], offs)
         nc.sync.dma_start(slot_sb[:], slot)
-        nc.sync.dma_start(factor_rows[0:64, :], old[0:8, :].rearrange("r (c i) -> (r c) i", i=P))
-        nc.sync.dma_start(factor_rows[64:128, :], new[0:8, :].rearrange("r (c i) -> (r c) i", i=P))
-        nc.sync.dma_start(scales[0:P:8, :].bitcast(I32), x_scales[0].bitcast(I32))
+        nc.sync.dma_start(factor_rows[OLD_ROW:NEW_ROW, :], old[0:1, :].rearrange("r (c i) -> (r c) i", i=P))
+        nc.sync.dma_start(factor_rows[NEW_ROW:P, :], new[0:1, :].rearrange("r (c i) -> (r c) i", i=P))
+        nc.sync.dma_start(scales[32:96:4, :].bitcast(I32), x_scales[0].bitcast(I32))
         nc.sync.dma_start(memory[0][:], mem[0:P, :])
         nc.sync.dma_start(words[:].bitcast(I32), x_words[0].rearrange("p n t -> p (n t)").bitcast(I32))
         nc.sync.dma_start(memory[1][:], mem[P : 2 * P, :])
 
         halves = range(S // HALF)
-        mixing = [psum.tile([P, HALF], F32, name=f"mixing{h}") for h in halves]
-        totals = [psum.tile([P, HALF], F32, name=f"total{h}") for h in halves]
-        product = [psum.tile([P, HALF], F32, name=f"product{i}") for i in range(2)]
+
+        def bank(tag, name):
+            return psum.tile([P, HALF], F32, name=name, tag=tag)
 
         factors = keep.tile([P, P], F32, name="factors")
-        nc.tensor.transpose(totals[0][:, 0:P], factor_rows[:], identity[:])
-        nc.scalar.copy(factors[:], totals[0][:, 0:P])
+        turned = bank("sum11", "turned_factors")
+        nc.tensor.transpose(turned[:, 0:P], factor_rows[:], identity[:])
+        nc.scalar.copy(factors[:], turned[:, 0:P])
 
         spread_scale = keep.tile([P, S], U8, name="spread_scale")
-        x_scale = keep.tile([P, S], U8, name="x_scale", align_bytes=64)
-        nc.vector.memset(x_scale[:].bitcast(I32), 0)
         nc.vector.tensor_copy(spread_scale[:], scales[:].indirect(offs_sb[:]))
         for r in range(4):
-            nc.scalar.dma_start(x_scale[r:P:32, :].bitcast(I32), spread_scale[8 * r : P : 32, :].bitcast(I32))
+            nc.scalar.dma_start(x_scale[r:P:32, :].bitcast(I32), spread_scale[32 + 4 * r : 96 : 16, :].bitcast(I32))
         picked = [[keep.tile([P, HALF], F32, name=f"picked{b}_{h}") for h in halves] for b in range(ROW_BLOCKS)]
-        kept = [keep.tile([P, S], F32, name=f"kept{b}") for b in range(ROW_BLOCKS)]
-        fresh = keep.tile([P, S], F32, name="fresh")
+        kept = [[keep.tile([P, HALF], F32, name=f"kept{b}_{h}") for h in halves] for b in range(ROW_BLOCKS)]
+        fresh = [[keep.tile([P, HALF], F32, name=f"fresh{b}_{h}") for h in halves] for b in range(ROW_BLOCKS)]
         x_codes = [keep.tile([P, HALF], U32, name=f"x_codes{h}", align_bytes=64) for h in halves]
         w_grouped = keep.tile([P, N, PACK], BF16, name="w_grouped", align_bytes=64)
         w_codes = keep.tile([P, N], U32, name="w_codes", tag="scales_then_w_codes", align_bytes=64)
         w_scale = keep.tile([P, N], U8, name="w_scale", align_bytes=64)
+        sums = [[bank(f"sum{b}{h}", f"sum{b}{h}") for h in halves] for b in range(ROW_BLOCKS)]
 
         def cols(i):
             return slice(i * P, (i + 1) * P)
@@ -88,17 +92,29 @@ def tile_picked_ema_none_p_kernel(
             for h in halves:
                 nc.vector.tensor_copy(picked[b][h][:], memory[b][:].indirect(list_half(slot_sb, h)))
 
+        def turn_back(b, h, terms, opens):
+            for c in range(PER_HALF):
+                nc.tensor.matmul(
+                    sums[b][h][:, cols(c)],
+                    terms[:, cols(c)],
+                    identity[:],
+                    start=opens and c == 0,
+                    stop=not opens and c == PER_HALF - 1,
+                    is_transpose=True,
+                )
+
         def scale_memory(b, h):
             for c in range(PER_HALF):
-                nc.tensor.transpose(mixing[h][:, cols(c)], picked[b][h][:, cols(c)], identity[:])
+                nc.tensor.transpose(sums[b][h][:, cols(c)], picked[b][h][:, cols(c)], identity[:])
             for c in range(PER_HALF):
-                chunk = h * PER_HALF + c
-                nc.scalar.activation(kept[b][:, cols(chunk)], mixing[h][:, cols(c)], COPY, scale=factors[:, chunk : chunk + 1])
+                column = OLD_ROW + h * PER_HALF + c
+                nc.scalar.activation(kept[b][h][:, cols(c)], sums[b][h][:, cols(c)], COPY, scale=factors[:, column : column + 1])
+            turn_back(b, h, kept[b][h], opens=True)
 
-        def project(b, h, bank, members):
+        def project(b, h, product, members):
             for c in members:
                 nc.tensor.matmul_mx(
-                    out=bank[:, cols(c)],
+                    out=product[:, cols(c)],
                     lhsT=x_codes[h][:, cols(c)].bitcast(FP8X4),
                     lhsT_scale=x_scale[:, cols(h * PER_HALF + c)],
                     rhs=w_codes[:, cols(b)].bitcast(FP8X4),
@@ -107,24 +123,13 @@ def tile_picked_ema_none_p_kernel(
                     stop=True,
                 )
             for c in members:
-                chunk = h * PER_HALF + c
-                nc.scalar.activation(fresh[:, cols(chunk)], bank[:, cols(c)], COPY, scale=factors[:, 64 + chunk : 64 + chunk + 1])
+                column = NEW_ROW + h * PER_HALF + c
+                nc.scalar.activation(fresh[b][h][:, cols(c)], product[:, cols(c)], COPY, scale=factors[:, column : column + 1])
 
-        def turn_back(bank, terms, opens):
-            for c in range(PER_HALF):
-                nc.tensor.matmul(
-                    bank[:, cols(c)], terms[c], identity[:], start=opens and c == 0, stop=not opens and c == PER_HALF - 1, is_transpose=True
-                )
-
-        def kept_terms(b, h):
-            return [kept[b][:, cols(h * PER_HALF + c)] for c in range(PER_HALF)]
-
-        def fresh_terms(h):
-            return [fresh[:, cols(h * PER_HALF + c)] for c in range(PER_HALF)]
-
-        def scatter(b, h, bank):
+        def scatter(b, h):
+            turn_back(b, h, fresh[b][h], opens=False)
             blended = keep.tile([P, HALF], F32, name=f"blended{b}_{h}")
-            nc.scalar.copy(blended[:], bank[:])
+            nc.scalar.copy(blended[:], sums[b][h][:])
             nc.vector.tensor_copy(memory[b][:].indirect(list_half(slot_sb, h)), blended[:])
 
         gather_memory(0)
@@ -132,24 +137,20 @@ def tile_picked_ema_none_p_kernel(
         nc.vector.quantize_mx(out=w_codes[:].bitcast(FP8X4), scales=w_scale[:], in_=w_grouped[:].rearrange("p n j -> p (n j)"))
         for h in halves:
             scale_memory(0, h)
-            turn_back(mixing[h], kept_terms(0, h), opens=True)
         for h in halves:
             nc.vector.tensor_copy(x_codes[h][:], words[:].indirect(list_half(offs_sb, h)))
         gather_memory(1)
 
-        project(0, 0, product[0], range(0, 2))
-        project(0, 0, product[1], range(2, 4))
-        turn_back(mixing[0], fresh_terms(0), opens=False)
-        scatter(0, 0, mixing[0])
-        project(0, 1, product[1], range(PER_HALF))
-        turn_back(mixing[1], fresh_terms(1), opens=False)
-        scatter(0, 1, mixing[1])
+        project(0, 0, bank("product0", "product00a"), range(0, 2))
+        project(0, 0, bank("product1", "product00b"), range(2, 4))
+        scatter(0, 0)
+        project(1, 0, bank("product2", "product10"), range(PER_HALF))
+        scale_memory(1, 0)
+        scatter(1, 0)
+        project(0, 1, bank("sum10", "product01"), range(PER_HALF))
+        scale_memory(1, 1)
+        scatter(0, 1)
         nc.sync.dma_start(out[0:P, :], memory[0][:])
-
-        for h in halves:
-            project(1, h, product[1], range(PER_HALF))
-            turn_back(totals[h], fresh_terms(h), opens=True)
-            scale_memory(1, h)
-            turn_back(totals[h], kept_terms(1, h), opens=False)
-            scatter(1, h, totals[h])
+        project(1, 1, bank("sum01", "product11"), range(PER_HALF))
+        scatter(1, 1)
         nc.sync.dma_start(out[P : 2 * P, :], memory[1][:])

@@ -14,6 +14,8 @@ U16 = mybir.dt.uint16
 U8 = mybir.dt.uint8
 FP8X4 = mybir.dt.float8_e4m3fn_x4
 COPY = mybir.ActivationFunctionType.Copy
+MULT = mybir.AluOpType.mult
+ADD = mybir.AluOpType.add
 
 P = 128
 PACK = 4
@@ -55,8 +57,8 @@ def tile_picked_ema_none_p_kernel(
         nc.sync.dma_start(factor_rows[OLD_ROW:NEW_ROW, :], old[0:1, :].rearrange("r (c i) -> (r c) i", i=P))
         nc.sync.dma_start(factor_rows[NEW_ROW:P, :], new[0:1, :].rearrange("r (c i) -> (r c) i", i=P))
         nc.sync.dma_start(scales[32:96:4, :].bitcast(I32), x_scales[0].bitcast(I32))
-        nc.sync.dma_start(memory[0][:], mem[0:P, :])
         nc.sync.dma_start(words[:].bitcast(I32), x_words[0].rearrange("p n t -> p (n t)").bitcast(I32))
+        nc.sync.dma_start(memory[0][:], mem[0:P, :])
         nc.sync.dma_start(memory[1][:], mem[P : 2 * P, :])
 
         halves = range(S // HALF)
@@ -65,7 +67,7 @@ def tile_picked_ema_none_p_kernel(
             return psum.tile([P, HALF], F32, name=name, tag=tag)
 
         factors = keep.tile([P, P], F32, name="factors")
-        turned = bank("sum11", "turned_factors")
+        turned = bank("back11", "turned_factors")
         nc.tensor.transpose(turned[:, 0:P], factor_rows[:], identity[:])
         nc.scalar.copy(factors[:], turned[:, 0:P])
 
@@ -73,46 +75,37 @@ def tile_picked_ema_none_p_kernel(
         nc.vector.tensor_copy(spread_scale[:], scales[:].indirect(offs_sb[:]))
         for r in range(4):
             nc.scalar.dma_start(x_scale[r:P:32, :].bitcast(I32), spread_scale[32 + 4 * r : 96 : 16, :].bitcast(I32))
-        picked = [[keep.tile([P, HALF], F32, name=f"picked{b}_{h}") for h in halves] for b in range(ROW_BLOCKS)]
-        kept = [[keep.tile([P, HALF], F32, name=f"kept{b}_{h}") for h in halves] for b in range(ROW_BLOCKS)]
-        fresh = [[keep.tile([P, HALF], F32, name=f"fresh{b}_{h}") for h in halves] for b in range(ROW_BLOCKS)]
+        kept = [keep.tile([P, S], F32, name=f"kept{b}") for b in range(ROW_BLOCKS)]
+        scaled = [[keep.tile([P, HALF], F32, name=f"scaled{b}_{h}") for h in halves] for b in range(ROW_BLOCKS)]
+        LEAD = 256
+        shared = keep.tile([P, 2 * S - LEAD], F32, name="shared")
+        old_row = shared[:, S - LEAD : 2 * S - LEAD]
+        fresh1 = keep.tile([P, S], F32, name="fresh1")
+        fresh = [shared[:, 0:S], fresh1[:]]
         x_codes = [keep.tile([P, HALF], U32, name=f"x_codes{h}", align_bytes=64) for h in halves]
         w_grouped = keep.tile([P, N, PACK], BF16, name="w_grouped", align_bytes=64)
         w_codes = keep.tile([P, N], U32, name="w_codes", tag="scales_then_w_codes", align_bytes=64)
         w_scale = keep.tile([P, N], U8, name="w_scale", align_bytes=64)
-        sums = [[bank(f"sum{b}{h}", f"sum{b}{h}") for h in halves] for b in range(ROW_BLOCKS)]
 
         def cols(i):
             return slice(i * P, (i + 1) * P)
 
+        def half_cols(h):
+            return slice(h * HALF, (h + 1) * HALF)
+
         def list_half(offsets, h):
             return offsets[:, h * HALF // STRIPE : (h + 1) * HALF // STRIPE]
 
-        def gather_memory(b):
-            for h in halves:
-                nc.vector.tensor_copy(picked[b][h][:], memory[b][:].indirect(list_half(slot_sb, h)))
-
-        def turn_back(b, h, terms, opens):
-            for c in range(PER_HALF):
-                nc.tensor.matmul(
-                    sums[b][h][:, cols(c)],
-                    terms[:, cols(c)],
-                    identity[:],
-                    start=opens and c == 0,
-                    stop=not opens and c == PER_HALF - 1,
-                    is_transpose=True,
-                )
-
-        def scale_memory(b, h):
-            for c in range(PER_HALF):
-                nc.tensor.transpose(sums[b][h][:, cols(c)], picked[b][h][:, cols(c)], identity[:])
+        for h in halves:
+            spread = bank(f"back0{h}", f"spread{h}")
             for c in range(PER_HALF):
                 column = OLD_ROW + h * PER_HALF + c
-                nc.scalar.activation(kept[b][h][:, cols(c)], sums[b][h][:, cols(c)], COPY, scale=factors[:, column : column + 1])
-            turn_back(b, h, kept[b][h], opens=True)
+                nc.tensor.transpose(spread[:, cols(c)], factors[:, column : column + 1].to_broadcast([P, P]), identity[:])
+            nc.scalar.copy(old_row[:, half_cols(h)], spread[:])
 
-        def project(b, h, product, members):
-            for c in members:
+        def project(b, h):
+            product = bank(f"product{b}{h}", f"product{b}{h}")
+            for c in range(PER_HALF):
                 nc.tensor.matmul_mx(
                     out=product[:, cols(c)],
                     lhsT=x_codes[h][:, cols(c)].bitcast(FP8X4),
@@ -122,35 +115,23 @@ def tile_picked_ema_none_p_kernel(
                     start=True,
                     stop=True,
                 )
-            for c in members:
+            for c in range(PER_HALF):
                 column = NEW_ROW + h * PER_HALF + c
-                nc.scalar.activation(fresh[b][h][:, cols(c)], product[:, cols(c)], COPY, scale=factors[:, column : column + 1])
+                nc.scalar.activation(scaled[b][h][:, cols(c)], product[:, cols(c)], COPY, scale=factors[:, column : column + 1])
+            back = bank("back01" if b == 1 else f"back{b}{h}", f"back{b}{h}")
+            for c in range(PER_HALF):
+                nc.tensor.transpose(back[:, cols(c)], scaled[b][h][:, cols(c)], identity[:])
+            nc.scalar.copy(fresh[b][:, half_cols(h)], back[:])
 
-        def scatter(b, h):
-            turn_back(b, h, fresh[b][h], opens=False)
-            blended = keep.tile([P, HALF], F32, name=f"blended{b}_{h}")
-            nc.scalar.copy(blended[:], sums[b][h][:])
-            nc.vector.tensor_copy(memory[b][:].indirect(list_half(slot_sb, h)), blended[:])
-
-        gather_memory(0)
         nc.scalar.copy(w_grouped[:], w_raw[:].rearrange("p j n -> p n j"))
         nc.vector.quantize_mx(out=w_codes[:].bitcast(FP8X4), scales=w_scale[:], in_=w_grouped[:].rearrange("p n j -> p (n j)"))
         for h in halves:
-            scale_memory(0, h)
-        for h in halves:
             nc.vector.tensor_copy(x_codes[h][:], words[:].indirect(list_half(offs_sb, h)))
-        gather_memory(1)
-
-        project(0, 0, bank("product0", "product00a"), range(0, 2))
-        project(0, 0, bank("product1", "product00b"), range(2, 4))
-        scatter(0, 0)
-        project(1, 0, bank("product2", "product10"), range(PER_HALF))
-        scale_memory(1, 0)
-        scatter(1, 0)
-        project(0, 1, bank("sum10", "product01"), range(PER_HALF))
-        scale_memory(1, 1)
-        scatter(0, 1)
-        nc.sync.dma_start(out[0:P, :], memory[0][:])
-        project(1, 1, bank("sum01", "product11"), range(PER_HALF))
-        scatter(1, 1)
-        nc.sync.dma_start(out[P : 2 * P, :], memory[1][:])
+        nc.vector.tensor_tensor(kept[0][:], memory[0][:].indirect(slot_sb[:]), old_row, MULT)
+        for a, z in ((0, LEAD), (LEAD, S)):
+            nc.vector.tensor_tensor(kept[1][:, a:z], memory[1][:].indirect(slot_sb[:, a // STRIPE : z // STRIPE]), old_row[:, a:z], MULT)
+        for b in range(ROW_BLOCKS):
+            for h in halves:
+                project(b, h)
+            nc.vector.tensor_tensor(memory[b][:].indirect(slot_sb[:]), kept[b][:], fresh[b], ADD)
+            nc.sync.dma_start(out[cols(b), :], memory[b][:])

@@ -37,8 +37,8 @@ def tile_picked_ema_none_p_kernel(
         offs_sb = keep.tile([P, S // STRIPE], U16, name="offs_sb")
         slot_sb = keep.tile([P, S // STRIPE], U16, name="slot_sb")
         words = keep.tile([P, T], U32, name="words")
-        scales = keep.tile([P, T], U8, name="scales", tag="scales_then_w_codes", align_bytes=64)
-        memory = [keep.tile([P, U], F32, name=f"memory{b}") for b in range(ROW_BLOCKS)]
+        scales = keep.tile([P, T], U8, name="scales", tag="scales_then_memory1")
+        memory0 = keep.tile([P, U], F32, name="memory0")
         w_raw = keep.tile([P, PACK, N], F32, name="w_raw")
         factor_rows = keep.tile([P, P], F32, name="factor_rows")
         identity = keep.tile([P, P], F32, name="identity")
@@ -58,8 +58,7 @@ def tile_picked_ema_none_p_kernel(
         nc.sync.dma_start(factor_rows[NEW_ROW:P, :], new[0:1, :].rearrange("r (c i) -> (r c) i", i=P))
         nc.sync.dma_start(scales[32:96:4, :].bitcast(I32), x_scales[0].bitcast(I32))
         nc.sync.dma_start(words[:].bitcast(I32), x_words[0].rearrange("p n t -> p (n t)").bitcast(I32))
-        nc.sync.dma_start(memory[0][:], mem[0:P, :])
-        nc.sync.dma_start(memory[1][:], mem[P : 2 * P, :])
+        nc.sync.dma_start(memory0[:], mem[0:P, :])
 
         halves = range(S // HALF)
 
@@ -74,7 +73,10 @@ def tile_picked_ema_none_p_kernel(
         spread_scale = keep.tile([P, S], U8, name="spread_scale")
         nc.vector.tensor_copy(spread_scale[:], scales[:].indirect(offs_sb[:]))
         for r in range(4):
-            nc.scalar.dma_start(x_scale[r:P:32, :].bitcast(I32), spread_scale[32 + 4 * r : 96 : 16, :].bitcast(I32))
+            nc.sync.dma_start(x_scale[r:P:32, :].bitcast(I32), spread_scale[32 + 4 * r : 96 : 16, :].bitcast(I32))
+        memory1 = keep.tile([P, U], F32, name="memory1", tag="scales_then_memory1")
+        nc.sync.dma_start(memory1[:], mem[P : 2 * P, :])
+        memory = [memory0, memory1]
         kept = [keep.tile([P, S], F32, name=f"kept{b}") for b in range(ROW_BLOCKS)]
         scaled = [[keep.tile([P, HALF], F32, name=f"scaled{b}_{h}") for h in halves] for b in range(ROW_BLOCKS)]
         LEAD = 256
@@ -84,7 +86,7 @@ def tile_picked_ema_none_p_kernel(
         fresh = [shared[:, 0:S], fresh1[:]]
         x_codes = [keep.tile([P, HALF], U32, name=f"x_codes{h}", align_bytes=64) for h in halves]
         w_grouped = keep.tile([P, N, PACK], BF16, name="w_grouped", align_bytes=64)
-        w_codes = keep.tile([P, N], U32, name="w_codes", tag="scales_then_w_codes", align_bytes=64)
+        w_codes = keep.tile([P, N], U32, name="w_codes", align_bytes=64)
         w_scale = keep.tile([P, N], U8, name="w_scale", align_bytes=64)
 
         def cols(i):
@@ -104,7 +106,7 @@ def tile_picked_ema_none_p_kernel(
             nc.scalar.copy(old_row[:, half_cols(h)], spread[:])
 
         def project(b, h):
-            product = bank(f"product{b}{h}", f"product{b}{h}")
+            product = bank("back01" if b == 1 else f"product{h}", f"product{b}{h}")
             for c in range(PER_HALF):
                 nc.tensor.matmul_mx(
                     out=product[:, cols(c)],
@@ -118,7 +120,7 @@ def tile_picked_ema_none_p_kernel(
             for c in range(PER_HALF):
                 column = NEW_ROW + h * PER_HALF + c
                 nc.scalar.activation(scaled[b][h][:, cols(c)], product[:, cols(c)], COPY, scale=factors[:, column : column + 1])
-            back = bank("back01" if b == 1 else f"back{b}{h}", f"back{b}{h}")
+            back = bank(f"back{b}{h}", f"back{b}{h}")
             for c in range(PER_HALF):
                 nc.tensor.transpose(back[:, cols(c)], scaled[b][h][:, cols(c)], identity[:])
             nc.scalar.copy(fresh[b][:, half_cols(h)], back[:])

@@ -57,8 +57,8 @@ def tile_picked_ema_none_p_kernel(
         nc.sync.dma_start(factor_rows[OLD_ROW:NEW_ROW, :], old[0:1, :].rearrange("r (c i) -> (r c) i", i=P))
         nc.sync.dma_start(factor_rows[NEW_ROW:P, :], new[0:1, :].rearrange("r (c i) -> (r c) i", i=P))
         nc.sync.dma_start(scales[32:96:4, :].bitcast(I32), x_scales[0].bitcast(I32))
-        nc.sync.dma_start(words[:].bitcast(I32), x_words[0].rearrange("p n t -> p (n t)").bitcast(I32))
         nc.sync.dma_start(memory0[:], mem[0:P, :])
+        nc.sync.dma_start(words[:].bitcast(I32), x_words[0].rearrange("p n t -> p (n t)").bitcast(I32))
 
         halves = range(S // HALF)
 
@@ -66,7 +66,7 @@ def tile_picked_ema_none_p_kernel(
             return psum.tile([P, HALF], F32, name=name, tag=tag)
 
         factors = keep.tile([P, P], F32, name="factors")
-        turned = bank("back11", "turned_factors")
+        turned = bank("back", "turned_factors")
         nc.tensor.transpose(turned[:, 0:P], factor_rows[:], identity[:])
         nc.scalar.copy(factors[:], turned[:, 0:P])
 
@@ -78,12 +78,9 @@ def tile_picked_ema_none_p_kernel(
         nc.sync.dma_start(memory1[:], mem[P : 2 * P, :])
         memory = [memory0, memory1]
         kept = [keep.tile([P, S], F32, name=f"kept{b}") for b in range(ROW_BLOCKS)]
-        scaled = [[keep.tile([P, HALF], F32, name=f"scaled{b}_{h}") for h in halves] for b in range(ROW_BLOCKS)]
         LEAD = 256
-        shared = keep.tile([P, 2 * S - LEAD], F32, name="shared")
-        old_row = shared[:, S - LEAD : 2 * S - LEAD]
-        fresh1 = keep.tile([P, S], F32, name="fresh1")
-        fresh = [shared[:, 0:S], fresh1[:]]
+        old_tile = keep.tile([P, S], F32, name="old_tile")
+        old_row = old_tile[:]
         x_codes = [keep.tile([P, HALF], U32, name=f"x_codes{h}", align_bytes=64) for h in halves]
         w_grouped = keep.tile([P, N, PACK], BF16, name="w_grouped", align_bytes=64)
         w_codes = keep.tile([P, N], U32, name="w_codes", align_bytes=64)
@@ -99,41 +96,53 @@ def tile_picked_ema_none_p_kernel(
             return offsets[:, h * HALF // STRIPE : (h + 1) * HALF // STRIPE]
 
         for h in halves:
-            spread = bank(f"back0{h}", f"spread{h}")
+            spread = bank(f"spread{h}", f"spread{h}")
             for c in range(PER_HALF):
                 column = OLD_ROW + h * PER_HALF + c
                 nc.tensor.transpose(spread[:, cols(c)], factors[:, column : column + 1].to_broadcast([P, P]), identity[:])
             nc.scalar.copy(old_row[:, half_cols(h)], spread[:])
 
-        def project(b, h):
-            product = bank("back01" if b == 1 else f"product{h}", f"product{b}{h}")
-            for c in range(PER_HALF):
+        def project(b, chunks, tag, fresh):
+            product = bank(f"product_{tag}", f"product{b}_{chunks[0]}")
+            scaled = keep.tile([P, HALF], F32, name=f"scaled{b}_{chunks[0]}", tag=f"scaled_{tag}")
+            for i, c in enumerate(chunks):
                 nc.tensor.matmul_mx(
-                    out=product[:, cols(c)],
-                    lhsT=x_codes[h][:, cols(c)].bitcast(FP8X4),
-                    lhsT_scale=x_scale[:, cols(h * PER_HALF + c)],
+                    out=product[:, cols(i)],
+                    lhsT=x_codes[c // PER_HALF][:, cols(c % PER_HALF)].bitcast(FP8X4),
+                    lhsT_scale=x_scale[:, cols(c)],
                     rhs=w_codes[:, cols(b)].bitcast(FP8X4),
                     rhs_scale=w_scale[:, cols(b)],
                     start=True,
                     stop=True,
                 )
-            for c in range(PER_HALF):
-                column = NEW_ROW + h * PER_HALF + c
-                nc.scalar.activation(scaled[b][h][:, cols(c)], product[:, cols(c)], COPY, scale=factors[:, column : column + 1])
-            back = bank(f"back{b}{h}", f"back{b}{h}")
-            for c in range(PER_HALF):
-                nc.tensor.transpose(back[:, cols(c)], scaled[b][h][:, cols(c)], identity[:])
-            nc.scalar.copy(fresh[b][:, half_cols(h)], back[:])
+            for i, c in enumerate(chunks):
+                nc.scalar.activation(scaled[:, cols(i)], product[:, cols(i)], COPY, scale=factors[:, NEW_ROW + c : NEW_ROW + c + 1])
+            back = bank("back", f"back{b}_{chunks[0]}")
+            for i, c in enumerate(chunks):
+                nc.tensor.transpose(back[:, cols(i)], scaled[:, cols(i)], identity[:])
+            nc.scalar.copy(fresh, back[:, 0 : len(chunks) * P])
+
+        def scatter(b, a, z, fresh):
+            offsets = slot_sb[:, a // STRIPE : z // STRIPE]
+            nc.vector.tensor_tensor(memory[b][:].indirect(offsets), kept[b][:, a:z], fresh, ADD)
 
         nc.scalar.copy(w_grouped[:], w_raw[:].rearrange("p j n -> p n j"))
         nc.vector.quantize_mx(out=w_codes[:].bitcast(FP8X4), scales=w_scale[:], in_=w_grouped[:].rearrange("p n j -> p (n j)"))
+        nc.vector.tensor_tensor(kept[0][:], memory[0][:].indirect(slot_sb[:]), old_row, MULT)
         for h in halves:
             nc.vector.tensor_copy(x_codes[h][:], words[:].indirect(list_half(offs_sb, h)))
-        nc.vector.tensor_tensor(kept[0][:], memory[0][:].indirect(slot_sb[:]), old_row, MULT)
         for a, z in ((0, LEAD), (LEAD, S)):
             nc.vector.tensor_tensor(kept[1][:, a:z], memory[1][:].indirect(slot_sb[:, a // STRIPE : z // STRIPE]), old_row[:, a:z], MULT)
-        for b in range(ROW_BLOCKS):
-            for h in halves:
-                project(b, h)
-            nc.vector.tensor_tensor(memory[b][:].indirect(slot_sb[:]), kept[b][:], fresh[b], ADD)
-            nc.sync.dma_start(out[cols(b), :], memory[b][:])
+        fresh0 = keep.tile([P, S], F32, name="fresh0")
+        fresh1 = keep.tile([P, S], F32, name="fresh1")
+        project(0, range(0, 2), "short", old_row[:, 0:LEAD])
+        scatter(0, 0, LEAD, old_row[:, 0:LEAD])
+        project(1, range(0, 4), "long", fresh1[:, 0:HALF])
+        scatter(1, 0, HALF, fresh1[:, 0:HALF])
+        project(0, range(2, 4), "short", fresh0[:, LEAD:HALF])
+        project(0, range(4, 8), "long", fresh0[:, HALF:S])
+        scatter(0, LEAD, S, fresh0[:, LEAD:S])
+        nc.sync.dma_start(out[0:P, :], memory[0][:])
+        project(1, range(4, 8), "long", fresh1[:, HALF:S])
+        scatter(1, HALF, S, fresh1[:, HALF:S])
+        nc.sync.dma_start(out[P : 2 * P, :], memory[1][:])

@@ -78,9 +78,10 @@ def tile_picked_ema_none_p_kernel(
         nc.sync.dma_start(memory1[:], mem[P : 2 * P, :])
         memory = [memory0, memory1]
         kept = [keep.tile([P, S], F32, name=f"kept{b}") for b in range(ROW_BLOCKS)]
-        LEAD = 256
-        old_tile = keep.tile([P, S], F32, name="old_tile")
-        old_row = old_tile[:]
+        LEAD = 128
+        TAIL = S - LEAD - P
+        old_tile = keep.tile([P, S + HALF - P], F32, name="old_tile")
+        old_row = old_tile[:, 0:S]
         x_codes = [keep.tile([P, HALF], U32, name=f"x_codes{h}", align_bytes=64) for h in halves]
         w_grouped = keep.tile([P, N, PACK], BF16, name="w_grouped", align_bytes=64)
         w_codes = keep.tile([P, N], U32, name="w_codes", align_bytes=64)
@@ -102,24 +103,27 @@ def tile_picked_ema_none_p_kernel(
                 nc.tensor.transpose(spread[:, cols(c)], factors[:, column : column + 1].to_broadcast([P, P]), identity[:])
             nc.scalar.copy(old_row[:, half_cols(h)], spread[:])
 
-        def project(b, chunks, tag, fresh):
-            product = bank(f"product_{tag}", f"product{b}_{chunks[0]}")
-            scaled = keep.tile([P, HALF], F32, name=f"scaled{b}_{chunks[0]}", tag=f"scaled_{tag}")
+        scaled = [keep.tile([P, N], F32, name=f"scaled{c}") for c in range(CHUNKS)]
+
+        def project(chunks, tag):
+            product = bank(tag, f"product{chunks[0]}")
             for i, c in enumerate(chunks):
                 nc.tensor.matmul_mx(
-                    out=product[:, cols(i)],
+                    out=product[:, i * N : (i + 1) * N],
                     lhsT=x_codes[c // PER_HALF][:, cols(c % PER_HALF)].bitcast(FP8X4),
                     lhsT_scale=x_scale[:, cols(c)],
-                    rhs=w_codes[:, cols(b)].bitcast(FP8X4),
-                    rhs_scale=w_scale[:, cols(b)],
+                    rhs=w_codes[:].bitcast(FP8X4),
+                    rhs_scale=w_scale[:],
                     start=True,
                     stop=True,
                 )
             for i, c in enumerate(chunks):
-                nc.scalar.activation(scaled[:, cols(i)], product[:, cols(i)], COPY, scale=factors[:, NEW_ROW + c : NEW_ROW + c + 1])
-            back = bank("back", f"back{b}_{chunks[0]}")
+                nc.scalar.activation(scaled[c][:], product[:, i * N : (i + 1) * N], COPY, scale=factors[:, NEW_ROW + c : NEW_ROW + c + 1])
+
+        def turn_back(b, chunks, tag, fresh):
+            back = bank(tag, f"back{b}_{chunks[0]}")
             for i, c in enumerate(chunks):
-                nc.tensor.transpose(back[:, cols(i)], scaled[:, cols(i)], identity[:])
+                nc.tensor.transpose(back[:, cols(i)], scaled[c][:, cols(b)], identity[:])
             nc.scalar.copy(fresh, back[:, 0 : len(chunks) * P])
 
         def scatter(b, a, z, fresh):
@@ -131,18 +135,24 @@ def tile_picked_ema_none_p_kernel(
         nc.vector.tensor_tensor(kept[0][:], memory[0][:].indirect(slot_sb[:]), old_row, MULT)
         for h in halves:
             nc.vector.tensor_copy(x_codes[h][:], words[:].indirect(list_half(offs_sb, h)))
-        for a, z in ((0, LEAD), (LEAD, S)):
+        for a, z in ((TAIL, S), (0, TAIL)):
             nc.vector.tensor_tensor(kept[1][:, a:z], memory[1][:].indirect(slot_sb[:, a // STRIPE : z // STRIPE]), old_row[:, a:z], MULT)
         fresh0 = keep.tile([P, S], F32, name="fresh0")
         fresh1 = keep.tile([P, S], F32, name="fresh1")
-        project(0, range(0, 2), "short", old_row[:, 0:LEAD])
-        scatter(0, 0, LEAD, old_row[:, 0:LEAD])
-        project(1, range(0, 4), "long", fresh1[:, 0:HALF])
-        scatter(1, 0, HALF, fresh1[:, 0:HALF])
-        project(0, range(2, 4), "short", fresh0[:, LEAD:HALF])
-        project(0, range(4, 8), "long", fresh0[:, HALF:S])
+        first0 = old_tile[:, TAIL : TAIL + LEAD]
+        first1 = old_tile[:, TAIL + LEAD : TAIL + LEAD + HALF]
+        project(range(0, 2), "product0")
+        turn_back(0, range(0, 1), "back", first0)
+        scatter(0, 0, LEAD, first0)
+        project(range(2, 4), "product1")
+        turn_back(1, range(0, 4), "back1", first1)
+        scatter(1, 0, HALF, first1)
+        turn_back(0, range(1, 4), "back", fresh0[:, LEAD:HALF])
+        project(range(4, 6), "back1")
+        project(range(6, 8), "back")
+        turn_back(0, range(4, 8), "product0", fresh0[:, HALF:S])
         scatter(0, LEAD, S, fresh0[:, LEAD:S])
         nc.sync.dma_start(out[0:P, :], memory[0][:])
-        project(1, range(4, 8), "long", fresh1[:, HALF:S])
+        turn_back(1, range(4, 8), "product1", fresh1[:, HALF:S])
         scatter(1, HALF, S, fresh1[:, HALF:S])
         nc.sync.dma_start(out[P : 2 * P, :], memory[1][:])

@@ -37,8 +37,8 @@ def tile_picked_ema_none_p_kernel(
         offs_sb = keep.tile([P, S // STRIPE], U16, name="offs_sb")
         slot_sb = keep.tile([P, S // STRIPE], U16, name="slot_sb")
         words = keep.tile([P, T], U32, name="words")
-        scales = keep.tile([P, T], U8, name="scales", tag="scales_then_memory1")
-        memory0 = keep.tile([P, U], F32, name="memory0")
+        scales = keep.tile([P, T], U8, name="scales")
+        memory = [keep.tile([P, U], F32, name=f"memory{b}") for b in range(ROW_BLOCKS)]
         w_raw = keep.tile([P, PACK, N], F32, name="w_raw")
         factor_rows = keep.tile([P, P], F32, name="factor_rows")
         identity = keep.tile([P, P], F32, name="identity")
@@ -57,16 +57,18 @@ def tile_picked_ema_none_p_kernel(
         nc.sync.dma_start(factor_rows[OLD_ROW:NEW_ROW, :], old[0:1, :].rearrange("r (c i) -> (r c) i", i=P))
         nc.sync.dma_start(factor_rows[NEW_ROW:P, :], new[0:1, :].rearrange("r (c i) -> (r c) i", i=P))
         nc.sync.dma_start(scales[32:96:4, :].bitcast(I32), x_scales[0].bitcast(I32))
-        nc.sync.dma_start(memory0[:], mem[0:P, :])
+        nc.sync.dma_start(memory[0][:], mem[0:P, :])
         nc.sync.dma_start(words[:].bitcast(I32), x_words[0].rearrange("p n t -> p (n t)").bitcast(I32))
+        nc.sync.dma_start(memory[1][:], mem[P : 2 * P, :])
 
-        halves = range(S // HALF)
+        def bank(number, name):
+            return psum.tile([P, HALF], F32, name=name, tag=f"bank{number}")
 
-        def bank(tag, name):
-            return psum.tile([P, HALF], F32, name=name, tag=tag)
+        def cols(i):
+            return slice(i * P, (i + 1) * P)
 
         factors = keep.tile([P, P], F32, name="factors")
-        turned = bank("back", "turned_factors")
+        turned = bank(0, "turned_factors")
         nc.tensor.transpose(turned[:, 0:P], factor_rows[:], identity[:])
         nc.scalar.copy(factors[:], turned[:, 0:P])
 
@@ -74,85 +76,77 @@ def tile_picked_ema_none_p_kernel(
         nc.vector.tensor_copy(spread_scale[:], scales[:].indirect(offs_sb[:]))
         for r in range(4):
             nc.sync.dma_start(x_scale[r:P:32, :].bitcast(I32), spread_scale[32 + 4 * r : 96 : 16, :].bitcast(I32))
-        memory1 = keep.tile([P, U], F32, name="memory1", tag="scales_then_memory1")
-        nc.sync.dma_start(memory1[:], mem[P : 2 * P, :])
-        memory = [memory0, memory1]
+
         kept = [keep.tile([P, S], F32, name=f"kept{b}") for b in range(ROW_BLOCKS)]
-        LEAD = 128
-        TAIL = S - LEAD - P
-        old_tile = keep.tile([P, S + HALF - P], F32, name="old_tile")
-        old_row = old_tile[:, 0:S]
-        x_codes = [keep.tile([P, HALF], U32, name=f"x_codes{h}", align_bytes=64) for h in halves]
+        old_row = keep.tile([P, S], F32, name="old_row")
+        x_codes = keep.tile([P, S], U32, name="x_codes", align_bytes=64)
         w_grouped = keep.tile([P, N, PACK], BF16, name="w_grouped", align_bytes=64)
         w_codes = keep.tile([P, N], U32, name="w_codes", align_bytes=64)
         w_scale = keep.tile([P, N], U8, name="w_scale", align_bytes=64)
 
-        def cols(i):
-            return slice(i * P, (i + 1) * P)
-
-        def half_cols(h):
-            return slice(h * HALF, (h + 1) * HALF)
-
-        def list_half(offsets, h):
-            return offsets[:, h * HALF // STRIPE : (h + 1) * HALF // STRIPE]
-
-        for h in halves:
-            spread = bank(f"spread{h}", f"spread{h}")
+        for h in range(S // HALF):
+            spread = bank(1 + h, f"spread{h}")
             for c in range(PER_HALF):
                 column = OLD_ROW + h * PER_HALF + c
                 nc.tensor.transpose(spread[:, cols(c)], factors[:, column : column + 1].to_broadcast([P, P]), identity[:])
-            nc.scalar.copy(old_row[:, half_cols(h)], spread[:])
+            nc.scalar.copy(old_row[:, h * HALF : (h + 1) * HALF], spread[:])
 
         scaled = [keep.tile([P, N], F32, name=f"scaled{c}") for c in range(CHUNKS)]
+        fresh = [keep.tile([P, S], F32, name=f"fresh{b}") for b in range(ROW_BLOCKS)]
 
-        def project(chunks, tag):
-            product = bank(tag, f"product{chunks[0]}")
-            for i, c in enumerate(chunks):
+        def project(parts, number):
+            product = bank(number, f"product{number}_{parts[0][0]}")
+            places = []
+            at = 0
+            for c, rows in parts:
+                place = product[:, at : at + rows.stop - rows.start]
+                at += rows.stop - rows.start
+                places.append(place)
                 nc.tensor.matmul_mx(
-                    out=product[:, i * N : (i + 1) * N],
-                    lhsT=x_codes[c // PER_HALF][:, cols(c % PER_HALF)].bitcast(FP8X4),
+                    out=place,
+                    lhsT=x_codes[:, cols(c)].bitcast(FP8X4),
                     lhsT_scale=x_scale[:, cols(c)],
-                    rhs=w_codes[:].bitcast(FP8X4),
-                    rhs_scale=w_scale[:],
+                    rhs=w_codes[:, rows].bitcast(FP8X4),
+                    rhs_scale=w_scale[:, rows],
                     start=True,
                     stop=True,
                 )
-            for i, c in enumerate(chunks):
-                nc.scalar.activation(scaled[c][:], product[:, i * N : (i + 1) * N], COPY, scale=factors[:, NEW_ROW + c : NEW_ROW + c + 1])
+            for (c, rows), place in zip(parts, places):
+                nc.scalar.activation(scaled[c][:, rows], place, COPY, scale=factors[:, NEW_ROW + c : NEW_ROW + c + 1])
 
-        def turn_back(b, chunks, tag, fresh):
-            back = bank(tag, f"back{b}_{chunks[0]}")
+        both = slice(0, N)
+
+        def turn_back(b, chunks, number):
+            back = bank(number, f"back{b}_{chunks[0]}")
             for i, c in enumerate(chunks):
                 nc.tensor.transpose(back[:, cols(i)], scaled[c][:, cols(b)], identity[:])
-            nc.scalar.copy(fresh, back[:, 0 : len(chunks) * P])
+            nc.scalar.copy(fresh[b][:, chunks[0] * P : (chunks[-1] + 1) * P], back[:, 0 : len(chunks) * P])
 
-        def scatter(b, a, z, fresh):
+        def scatter(b, chunks):
+            a, z = chunks[0] * P, (chunks[-1] + 1) * P
             offsets = slot_sb[:, a // STRIPE : z // STRIPE]
-            nc.vector.tensor_tensor(memory[b][:].indirect(offsets), kept[b][:, a:z], fresh, ADD)
+            nc.vector.tensor_tensor(memory[b][:].indirect(offsets), kept[b][:, a:z], fresh[b][:, a:z], ADD)
 
         nc.scalar.copy(w_grouped[:], w_raw[:].rearrange("p j n -> p n j"))
         nc.vector.quantize_mx(out=w_codes[:].bitcast(FP8X4), scales=w_scale[:], in_=w_grouped[:].rearrange("p n j -> p (n j)"))
-        nc.vector.tensor_tensor(kept[0][:], memory[0][:].indirect(slot_sb[:]), old_row, MULT)
-        for h in halves:
-            nc.vector.tensor_copy(x_codes[h][:], words[:].indirect(list_half(offs_sb, h)))
-        for a, z in ((TAIL, S), (0, TAIL)):
-            nc.vector.tensor_tensor(kept[1][:, a:z], memory[1][:].indirect(slot_sb[:, a // STRIPE : z // STRIPE]), old_row[:, a:z], MULT)
-        fresh0 = keep.tile([P, S], F32, name="fresh0")
-        fresh1 = keep.tile([P, S], F32, name="fresh1")
-        first0 = old_tile[:, TAIL : TAIL + LEAD]
-        first1 = old_tile[:, TAIL + LEAD : TAIL + LEAD + HALF]
-        project(range(0, 2), "product0")
-        turn_back(0, range(0, 1), "back", first0)
-        scatter(0, 0, LEAD, first0)
-        project(range(2, 4), "product1")
-        turn_back(1, range(0, 4), "back1", first1)
-        scatter(1, 0, HALF, first1)
-        turn_back(0, range(1, 4), "back", fresh0[:, LEAD:HALF])
-        project(range(4, 6), "back1")
-        project(range(6, 8), "back")
-        turn_back(0, range(4, 8), "product0", fresh0[:, HALF:S])
-        scatter(0, LEAD, S, fresh0[:, LEAD:S])
-        nc.sync.dma_start(out[0:P, :], memory[0][:])
-        turn_back(1, range(4, 8), "product1", fresh1[:, HALF:S])
-        scatter(1, HALF, S, fresh1[:, HALF:S])
+        nc.vector.tensor_tensor(kept[0][:], memory[0][:].indirect(slot_sb[:]), old_row[:], MULT)
+        nc.vector.tensor_copy(x_codes[:], words[:].indirect(offs_sb[:]))
+        nc.vector.tensor_tensor(kept[1][:], memory[1][:].indirect(slot_sb[:]), old_row[:], MULT)
+        project([(0, cols(0))], 0)
+        turn_back(0, range(0, 1), 5)
+        scatter(0, range(0, 1))
+        project([(0, cols(1)), (1, both)], 1)
+        turn_back(1, range(0, 2), 6)
+        scatter(1, range(0, 2))
+        project([(2, both), (3, both)], 2)
+        turn_back(0, range(1, 4), 7)
+        scatter(0, range(1, 4))
+        project([(4, both), (5, both)], 5)
+        turn_back(1, range(2, 4), 0)
+        project([(6, both), (7, both)], 6)
+        turn_back(1, range(4, 8), 1)
+        scatter(1, range(2, 8))
         nc.sync.dma_start(out[P : 2 * P, :], memory[1][:])
+        turn_back(0, range(4, 8), 2)
+        scatter(0, range(4, 8))
+        nc.sync.dma_start(out[0:P, :], memory[0][:])

@@ -79,7 +79,7 @@ def tile_picked_ema_none_p_kernel(
 
         kept = [keep.tile([P, S], F32, name=f"kept{b}") for b in range(ROW_BLOCKS)]
         old_row = keep.tile([P, S], F32, name="old_row")
-        x_codes = keep.tile([P, S], U32, name="x_codes", align_bytes=64)
+        x_codes = [keep.tile([P, HALF], U32, name=f"x_codes{h}", align_bytes=64) for h in range(S // HALF)]
         w_grouped = keep.tile([P, N, PACK], BF16, name="w_grouped", align_bytes=64)
         w_codes = keep.tile([P, N], U32, name="w_codes", align_bytes=64)
         w_scale = keep.tile([P, N], U8, name="w_scale", align_bytes=64)
@@ -104,7 +104,7 @@ def tile_picked_ema_none_p_kernel(
                 places.append(place)
                 nc.tensor.matmul_mx(
                     out=place,
-                    lhsT=x_codes[:, cols(c)].bitcast(FP8X4),
+                    lhsT=x_codes[c // PER_HALF][:, cols(c % PER_HALF)].bitcast(FP8X4),
                     lhsT_scale=x_scale[:, cols(c)],
                     rhs=w_codes[:, rows].bitcast(FP8X4),
                     rhs_scale=w_scale[:, rows],
@@ -130,7 +130,8 @@ def tile_picked_ema_none_p_kernel(
         nc.scalar.copy(w_grouped[:], w_raw[:].rearrange("p j n -> p n j"))
         nc.vector.quantize_mx(out=w_codes[:].bitcast(FP8X4), scales=w_scale[:], in_=w_grouped[:].rearrange("p n j -> p (n j)"))
         nc.vector.tensor_tensor(kept[0][:], memory[0][:].indirect(slot_sb[:]), old_row[:], MULT)
-        nc.vector.tensor_copy(x_codes[:], words[:].indirect(offs_sb[:]))
+        for h in range(S // HALF):
+            nc.vector.tensor_copy(x_codes[h][:], words[:].indirect(offs_sb[:, h * HALF // STRIPE : (h + 1) * HALF // STRIPE]))
         nc.vector.tensor_tensor(kept[1][:], memory[1][:].indirect(slot_sb[:]), old_row[:], MULT)
         project([(0, cols(0))], 0)
         turn_back(0, range(0, 1), 5)

@@ -37,8 +37,8 @@ def tile_picked_ema_none_p_kernel(
         offs_sb = keep.tile([P, S // STRIPE], U16, name="offs_sb")
         slot_sb = keep.tile([P, S // STRIPE], U16, name="slot_sb")
         words = keep.tile([P, T], U32, name="words")
-        scales = keep.tile([P, T], U8, name="scales")
-        memory = [keep.tile([P, U], F32, name=f"memory{b}") for b in range(ROW_BLOCKS)]
+        scales = keep.tile([P, T], U8, name="scales", tag="scales_then_memory")
+        memory = [keep.tile([P, U], F32, name="memory0")]
         w_raw = keep.tile([P, PACK, N], F32, name="w_raw")
         factor_rows = keep.tile([P, P], F32, name="factor_rows")
         identity = keep.tile([P, P], F32, name="identity")
@@ -59,95 +59,130 @@ def tile_picked_ema_none_p_kernel(
         nc.sync.dma_start(scales[32:96:4, :].bitcast(I32), x_scales[0].bitcast(I32))
         nc.sync.dma_start(memory[0][:], mem[0:P, :])
         nc.sync.dma_start(words[:].bitcast(I32), x_words[0].rearrange("p n t -> p (n t)").bitcast(I32))
+
+        spread_scale = keep.tile([P, S], U8, name="spread_scale")
+        nc.vector.tensor_copy(spread_scale[:], scales[:].indirect(offs_sb[:]))
+        for r in range(4):
+            nc.sync.dma_start(x_scale[r:P:32, :].bitcast(I32), spread_scale[32 + 4 * r : 96 : 16, :].bitcast(I32))
+        memory.append(keep.tile([P, U], F32, name="memory1", tag="scales_then_memory"))
         nc.sync.dma_start(memory[1][:], mem[P : 2 * P, :])
 
         def bank(number, name):
             return psum.tile([P, HALF], F32, name=name, tag=f"bank{number}")
 
-        def cols(i):
-            return slice(i * P, (i + 1) * P)
+        def cols(i, width=P):
+            return slice(i * width, (i + 1) * width)
+
+        def slots(entries):
+            return slot_sb[:, entries.start // STRIPE : entries.stop // STRIPE]
+
+        first, second = cols(0, HALF), cols(1, HALF)
 
         factors = keep.tile([P, P], F32, name="factors")
         turned = bank(0, "turned_factors")
         nc.tensor.transpose(turned[:, 0:P], factor_rows[:], identity[:])
         nc.scalar.copy(factors[:], turned[:, 0:P])
 
-        spread_scale = keep.tile([P, S], U8, name="spread_scale")
-        nc.vector.tensor_copy(spread_scale[:], scales[:].indirect(offs_sb[:]))
-        for r in range(4):
-            nc.sync.dma_start(x_scale[r:P:32, :].bitcast(I32), spread_scale[32 + 4 * r : 96 : 16, :].bitcast(I32))
-
-        kept = [keep.tile([P, S], F32, name=f"kept{b}") for b in range(ROW_BLOCKS)]
-        old_row = keep.tile([P, S], F32, name="old_row")
-        x_codes = [keep.tile([P, HALF], U32, name=f"x_codes{h}", align_bytes=64) for h in range(S // HALF)]
         w_grouped = keep.tile([P, N, PACK], BF16, name="w_grouped", align_bytes=64)
         w_codes = keep.tile([P, N], U32, name="w_codes", align_bytes=64)
         w_scale = keep.tile([P, N], U8, name="w_scale", align_bytes=64)
-
-        for h in range(S // HALF):
-            spread = bank(1 + h, f"spread{h}")
-            for c in range(PER_HALF):
-                column = OLD_ROW + h * PER_HALF + c
-                nc.tensor.transpose(spread[:, cols(c)], factors[:, column : column + 1].to_broadcast([P, P]), identity[:])
-            nc.scalar.copy(old_row[:, h * HALF : (h + 1) * HALF], spread[:])
-
-        scaled = [keep.tile([P, N], F32, name=f"scaled{c}") for c in range(CHUNKS)]
-        fresh = [keep.tile([P, S], F32, name=f"fresh{b}") for b in range(ROW_BLOCKS)]
-
-        def project(parts, number):
-            product = bank(number, f"product{number}_{parts[0][0]}")
-            places = []
-            at = 0
-            for c, rows in parts:
-                place = product[:, at : at + rows.stop - rows.start]
-                at += rows.stop - rows.start
-                places.append(place)
-                nc.tensor.matmul_mx(
-                    out=place,
-                    lhsT=x_codes[c // PER_HALF][:, cols(c % PER_HALF)].bitcast(FP8X4),
-                    lhsT_scale=x_scale[:, cols(c)],
-                    rhs=w_codes[:, rows].bitcast(FP8X4),
-                    rhs_scale=w_scale[:, rows],
-                    start=True,
-                    stop=True,
-                )
-            for (c, rows), place in zip(parts, places):
-                nc.scalar.activation(scaled[c][:, rows], place, COPY, scale=factors[:, NEW_ROW + c : NEW_ROW + c + 1])
-
-        both = slice(0, N)
-
-        def turn_back(b, chunks, number):
-            back = bank(number, f"back{b}_{chunks[0]}")
-            for i, c in enumerate(chunks):
-                nc.tensor.transpose(back[:, cols(i)], scaled[c][:, cols(b)], identity[:])
-            nc.scalar.copy(fresh[b][:, chunks[0] * P : (chunks[-1] + 1) * P], back[:, 0 : len(chunks) * P])
-
-        def scatter(b, chunks):
-            a, z = chunks[0] * P, (chunks[-1] + 1) * P
-            offsets = slot_sb[:, a // STRIPE : z // STRIPE]
-            nc.vector.tensor_tensor(memory[b][:].indirect(offsets), kept[b][:, a:z], fresh[b][:, a:z], ADD)
-
         nc.scalar.copy(w_grouped[:], w_raw[:].rearrange("p j n -> p n j"))
         nc.vector.quantize_mx(out=w_codes[:].bitcast(FP8X4), scales=w_scale[:], in_=w_grouped[:].rearrange("p n j -> p (n j)"))
-        nc.vector.tensor_tensor(kept[0][:], memory[0][:].indirect(slot_sb[:]), old_row[:], MULT)
+
+        def spread_row(name, row, places, number):
+            for h, place in enumerate(places):
+                wide = bank(number + h, f"{name}{h}")
+                for c in range(PER_HALF):
+                    column = row + h * PER_HALF + c
+                    nc.tensor.transpose(wide[:, cols(c)], factors[:, column : column + 1].to_broadcast([P, P]), identity[:])
+                nc.scalar.copy(place, wide[:])
+
+        line = keep.tile([P, 3 * HALF], F32, name="line")
+        old_row = [line[:, cols(0, HALF)], line[:, cols(2, HALF)]]
+        fresh = line[:, HALF : 3 * HALF]
+        new_row = keep.tile([P, S], F32, name="new_row")
+        spread_row("old_row", OLD_ROW, old_row, 1)
+        spread_row("new_row", NEW_ROW, [new_row[:, first], new_row[:, second]], 3)
+
+        kept = [keep.tile([P, S], F32, name=f"kept{b}") for b in range(ROW_BLOCKS)]
+
+        def look_up(b, h):
+            entries = cols(h, HALF)
+            nc.vector.tensor_tensor(kept[b][:, entries], memory[b][:].indirect(slots(entries)), old_row[h], MULT)
+
+        kept_turned = keep.tile([P, S], F32, name="kept_turned")
         for h in range(S // HALF):
-            nc.vector.tensor_copy(x_codes[h][:], words[:].indirect(offs_sb[:, h * HALF // STRIPE : (h + 1) * HALF // STRIPE]))
-        nc.vector.tensor_tensor(kept[1][:], memory[1][:].indirect(slot_sb[:]), old_row[:], MULT)
-        project([(0, cols(0))], 0)
-        turn_back(0, range(0, 1), 5)
-        scatter(0, range(0, 1))
-        project([(0, cols(1)), (1, both)], 1)
-        turn_back(1, range(0, 2), 6)
-        scatter(1, range(0, 2))
-        project([(2, both), (3, both)], 2)
-        turn_back(0, range(1, 4), 7)
-        scatter(0, range(1, 4))
-        project([(4, both), (5, both)], 5)
-        turn_back(1, range(2, 4), 0)
-        project([(6, both), (7, both)], 6)
-        turn_back(1, range(4, 8), 1)
-        scatter(1, range(2, 8))
+            look_up(0, h)
+            wide = bank(5 + h, f"kept_wide{h}")
+            for c in range(PER_HALF):
+                nc.tensor.transpose(wide[:, cols(c)], kept[0][:, cols(h * PER_HALF + c)], identity[:])
+            nc.scalar.copy(kept_turned[:, cols(h, HALF)], wide[:])
+
+        x_codes = keep.tile([P, S], U32, name="x_codes", align_bytes=64)
+        for a, z in ((0, S // 4), (S // 4, HALF), (HALF, S)):
+            nc.vector.tensor_copy(x_codes[:, a:z], words[:].indirect(offs_sb[:, a // STRIPE : z // STRIPE]))
+
+        def multiply(place, stationary, moving):
+            (a_codes, a_scale), (b_codes, b_scale) = stationary, moving
+            nc.tensor.matmul_mx(
+                out=place,
+                lhsT=a_codes.bitcast(FP8X4),
+                lhsT_scale=a_scale,
+                rhs=b_codes.bitcast(FP8X4),
+                rhs_scale=b_scale,
+                start=True,
+                stop=True,
+            )
+
+        def picked(entries):
+            return x_codes[:, entries], x_scale[:, entries]
+
+        def weights(b):
+            return w_codes[:, cols(b)], w_scale[:, cols(b)]
+
+        scaled = keep.tile([P, S], F32, name="scaled")
+        blend = keep.tile([P, S], F32, name="blend")
+
+        def project(chunks, number):
+            product = bank(number, f"product{chunks[0]}")
+            for i, c in enumerate(chunks):
+                multiply(product[:, cols(i)], picked(cols(c)), weights(0))
+            for i, c in enumerate(chunks):
+                nc.scalar.activation(scaled[:, cols(c)], product[:, cols(i)], COPY, scale=factors[:, NEW_ROW + c : NEW_ROW + c + 1])
+
+        def turn_back(chunks, number):
+            back = bank(number, f"back{chunks[0]}")
+            for i, c in enumerate(chunks):
+                nc.tensor.matmul(back[:, cols(i)], kept_turned[:, cols(c)], identity[:], is_transpose=True, start=True, stop=False)
+                nc.tensor.matmul(back[:, cols(i)], scaled[:, cols(c)], identity[:], is_transpose=True, start=False, stop=True)
+            nc.scalar.copy(blend[:, chunks[0] * P : (chunks[-1] + 1) * P], back[:, 0 : len(chunks) * P])
+
+        def put(quarter):
+            entries = cols(quarter, S // 4)
+            nc.scalar.activation(memory[0][:].indirect(slots(entries)), blend[:, entries], COPY)
+
+        def scale_rows(h, number):
+            rows = bank(number, f"rows{h}")
+            multiply(rows[:], weights(1), picked(cols(h, HALF)))
+            return rows
+
+        project(range(0, 2), 0)
+        project(range(2, 4), 1)
+        rows = scale_rows(0, 3)
+        nc.vector.tensor_tensor(fresh[:, first], rows[:], new_row[:, first], MULT)
+        turn_back(range(0, 2), 5)
+        put(0)
+        turn_back(range(2, 4), 6)
+        project(range(4, 8), 5)
+        rows = scale_rows(1, 6)
+        put(1)
+        turn_back(range(4, 8), 7)
+        put(2)
+        put(3)
+        nc.scalar.dma_start(out[0:P, :], memory[0][:])
+
+        look_up(1, 1)
+        look_up(1, 0)
+        nc.vector.tensor_tensor(fresh[:, second], rows[:], new_row[:, second], MULT)
+        nc.vector.tensor_tensor(memory[1][:].indirect(slot_sb[:]), kept[1][:], fresh, ADD)
         nc.sync.dma_start(out[P : 2 * P, :], memory[1][:])
-        turn_back(0, range(4, 8), 2)
-        scatter(0, range(4, 8))
-        nc.sync.dma_start(out[0:P, :], memory[0][:])

@@ -55,7 +55,7 @@ def tile_picked_ema_none_p_kernel(
         nc.sync.dma_start(offs_sb[:], offs)
         nc.sync.dma_start(slot_sb[:], slot)
         nc.sync.dma_start(factor_rows[OLD_ROW:NEW_ROW, :], old[0:1, :].rearrange("r (c i) -> (r c) i", i=P))
-        nc.sync.dma_start(factor_rows[NEW_ROW:P, :], new[0:1, :].rearrange("r (c i) -> (r c) i", i=P))
+        nc.scalar.dma_start(factor_rows[NEW_ROW:P, :], new[0:1, :].rearrange("r (c i) -> (r c) i", i=P))
         nc.sync.dma_start(scales[32:96:4, :].bitcast(I32), x_scales[0].bitcast(I32))
         nc.sync.dma_start(memory[0][:], mem[0:P, :])
         nc.sync.dma_start(words[:].bitcast(I32), x_words[0].rearrange("p n t -> p (n t)").bitcast(I32))
@@ -97,9 +97,8 @@ def tile_picked_ema_none_p_kernel(
                     nc.tensor.transpose(wide[:, cols(c)], factors[:, column : column + 1].to_broadcast([P, P]), identity[:])
                 nc.scalar.copy(place, wide[:])
 
-        line = keep.tile([P, 3 * HALF], F32, name="line")
-        old_row = [line[:, cols(0, HALF)], line[:, cols(2, HALF)]]
-        fresh = line[:, HALF : 3 * HALF]
+        fresh = keep.tile([P, S], F32, name="old_then_fresh")
+        old_row = [fresh[:, first], fresh[:, second]]
         new_row = keep.tile([P, S], F32, name="new_row")
         spread_row("old_row", OLD_ROW, old_row, 1)
         spread_row("new_row", NEW_ROW, [new_row[:, first], new_row[:, second]], 3)
@@ -110,13 +109,19 @@ def tile_picked_ema_none_p_kernel(
             entries = cols(h, HALF)
             nc.vector.tensor_tensor(kept[b][:, entries], memory[b][:].indirect(slots(entries)), old_row[h], MULT)
 
-        kept_turned = keep.tile([P, S], F32, name="kept_turned")
-        for h in range(S // HALF):
-            look_up(0, h)
-            wide = bank(5 + h, f"kept_wide{h}")
-            for c in range(PER_HALF):
-                nc.tensor.transpose(wide[:, cols(c)], kept[0][:, cols(h * PER_HALF + c)], identity[:])
-            nc.scalar.copy(kept_turned[:, cols(h, HALF)], wide[:])
+        kept_turned = keep.tile([P, HALF], F32, name="kept_turned")
+        look_up(0, 0)
+        wide = bank(0, "kept_wide")
+        for c in range(PER_HALF):
+            nc.tensor.transpose(wide[:, cols(c)], kept[0][:, cols(c)], identity[:])
+        nc.scalar.copy(kept_turned[:], wide[:])
+        look_up(0, 1)
+
+        pieces = (range(0, 2), range(2, 4), range(4, 8))
+        back = [bank(5 + i, f"back{i}") for i in range(len(pieces))]
+        for chunks, sums in zip(pieces[:2], back):
+            for i, c in enumerate(chunks):
+                nc.tensor.matmul(sums[:, cols(i)], kept_turned[:, cols(c)], identity[:], is_transpose=True, start=i == 0, stop=False)
 
         x_codes = keep.tile([P, S], U32, name="x_codes", align_bytes=64)
         for a, z in ((0, S // 4), (S // 4, HALF), (HALF, S)):
@@ -141,7 +146,7 @@ def tile_picked_ema_none_p_kernel(
             return w_codes[:, cols(b)], w_scale[:, cols(b)]
 
         scaled = keep.tile([P, S], F32, name="scaled")
-        blend = keep.tile([P, S], F32, name="blend")
+        blend = keep.tile([P, HALF], F32, name="blend")
 
         def project(chunks, number):
             product = bank(number, f"product{chunks[0]}")
@@ -150,39 +155,38 @@ def tile_picked_ema_none_p_kernel(
             for i, c in enumerate(chunks):
                 nc.scalar.activation(scaled[:, cols(c)], product[:, cols(i)], COPY, scale=factors[:, NEW_ROW + c : NEW_ROW + c + 1])
 
-        def turn_back(chunks, number):
-            back = bank(number, f"back{chunks[0]}")
+        def turn_back(piece):
+            chunks = pieces[piece]
             for i, c in enumerate(chunks):
-                nc.tensor.matmul(back[:, cols(i)], kept_turned[:, cols(c)], identity[:], is_transpose=True, start=True, stop=False)
-                nc.tensor.matmul(back[:, cols(i)], scaled[:, cols(c)], identity[:], is_transpose=True, start=False, stop=True)
-            nc.scalar.copy(blend[:, chunks[0] * P : (chunks[-1] + 1) * P], back[:, 0 : len(chunks) * P])
+                nc.tensor.matmul(back[piece][:, cols(i)], scaled[:, cols(c)], identity[:], is_transpose=True, start=False, stop=c == chunks[-1])
+            nc.scalar.copy(blend[:, chunks[0] * P : (chunks[-1] + 1) * P], back[piece][:, 0 : len(chunks) * P])
 
-        def put(quarter):
-            entries = cols(quarter, S // 4)
-            nc.scalar.activation(memory[0][:].indirect(slots(entries)), blend[:, entries], COPY)
+        def put(quarter, sums):
+            nc.scalar.activation(memory[0][:].indirect(slots(cols(quarter, S // 4))), sums[:, cols(quarter % 2, S // 4)], COPY)
 
         def scale_rows(h, number):
             rows = bank(number, f"rows{h}")
             multiply(rows[:], weights(1), picked(cols(h, HALF)))
             return rows
 
-        project(range(0, 2), 0)
-        project(range(2, 4), 1)
-        rows = scale_rows(0, 3)
-        nc.vector.tensor_tensor(fresh[:, first], rows[:], new_row[:, first], MULT)
-        turn_back(range(0, 2), 5)
-        put(0)
-        turn_back(range(2, 4), 6)
-        project(range(4, 8), 5)
-        rows = scale_rows(1, 6)
-        put(1)
-        turn_back(range(4, 8), 7)
-        put(2)
-        put(3)
-        nc.scalar.dma_start(out[0:P, :], memory[0][:])
+        project(pieces[0], 0)
+        project(pieces[1], 1)
+        turn_back(0)
+        put(0, blend)
+        project(pieces[2], 1)
+        turn_back(1)
+        rows = [scale_rows(0, 5), scale_rows(1, 0)]
+        put(1, blend)
+        for i, c in enumerate(pieces[2]):
+            nc.tensor.transpose(back[2][:, cols(i)], scaled[:, cols(c)], identity[:])
 
-        look_up(1, 1)
-        look_up(1, 0)
-        nc.vector.tensor_tensor(fresh[:, second], rows[:], new_row[:, second], MULT)
-        nc.vector.tensor_tensor(memory[1][:].indirect(slot_sb[:]), kept[1][:], fresh, ADD)
+        for h in range(S // HALF):
+            look_up(1, h)
+        for h in range(S // HALF):
+            nc.vector.tensor_tensor(fresh[:, cols(h, HALF)], rows[h][:], new_row[:, cols(h, HALF)], MULT)
+        nc.vector.tensor_tensor(new_row[:, first], back[2][:], kept[0][:, second], ADD)
+        put(2, new_row[:, first])
+        put(3, new_row[:, first])
+        nc.scalar.dma_start(out[0:P, :], memory[0][:])
+        nc.vector.tensor_tensor(memory[1][:].indirect(slot_sb[:]), kept[1][:], fresh[:], ADD)
         nc.sync.dma_start(out[P : 2 * P, :], memory[1][:])

@@ -24,6 +24,7 @@ HALF = 512
 CHUNKS = S // P
 PER_HALF = HALF // P
 ROW_BLOCKS = N // P
+QUARTER = S // 4
 
 
 def tile_picked_ema_none_p_kernel(
@@ -32,30 +33,32 @@ def tile_picked_ema_none_p_kernel(
     nc = tc.nc
     with ExitStack() as ctx:
         keep = ctx.enter_context(tc.tile_pool(name="keep", bufs=1))
+        shared = ctx.enter_context(tc.tile_pool(name="shared", bufs=1))
         psum = ctx.enter_context(tc.psum_pool(name="psum", bufs=1))
 
         offs_sb = keep.tile([P, S // STRIPE], U16, name="offs_sb")
         slot_sb = keep.tile([P, S // STRIPE], U16, name="slot_sb")
         words = keep.tile([P, T], U32, name="words")
-        scales = keep.tile([P, T], U8, name="scales", tag="scales_then_memory")
+        block_bytes = 4 * U
+        scales = shared.tile([P, T], U8, name="scales", offset=block_bytes - T // 2)
         memory = [keep.tile([P, U], F32, name="memory0")]
         w_raw = keep.tile([P, PACK, N], F32, name="w_raw")
         factor_rows = keep.tile([P, P], F32, name="factor_rows")
         identity = keep.tile([P, P], F32, name="identity")
         x_scale = keep.tile([P, S], U8, name="x_scale", align_bytes=64)
 
-        OLD_ROW = P - 2 * CHUNKS
-        NEW_ROW = P - CHUNKS
+        NEW_ROW = P - PER_HALF
+        OLD_ROW = NEW_ROW - CHUNKS
         nc.vector.memset(scales[:].bitcast(I32), 0)
         nc.vector.memset(x_scale[:].bitcast(I32), 0)
         nc.vector.memset(factor_rows[0:OLD_ROW, :], 0.0)
         make_identity(nc, identity[:])
 
+        nc.sync.dma_start(factor_rows[OLD_ROW:NEW_ROW, :], old[0:1, :].rearrange("r (c i) -> (r c) i", i=P))
         nc.sync.dma_start(w_raw[:], w1.rearrange("(p j) n -> p j n", j=PACK))
         nc.sync.dma_start(offs_sb[:], offs)
         nc.sync.dma_start(slot_sb[:], slot)
-        nc.sync.dma_start(factor_rows[OLD_ROW:NEW_ROW, :], old[0:1, :].rearrange("r (c i) -> (r c) i", i=P))
-        nc.scalar.dma_start(factor_rows[NEW_ROW:P, :], new[0:1, :].rearrange("r (c i) -> (r c) i", i=P))
+        nc.scalar.dma_start(factor_rows[NEW_ROW:P, :], new[0:1, 0:HALF].rearrange("r (c i) -> (r c) i", i=P))
         nc.sync.dma_start(scales[32:96:4, :].bitcast(I32), x_scales[0].bitcast(I32))
         nc.sync.dma_start(memory[0][:], mem[0:P, :])
         nc.sync.dma_start(words[:].bitcast(I32), x_words[0].rearrange("p n t -> p (n t)").bitcast(I32))
@@ -64,8 +67,11 @@ def tile_picked_ema_none_p_kernel(
         nc.vector.tensor_copy(spread_scale[:], scales[:].indirect(offs_sb[:]))
         for r in range(4):
             nc.sync.dma_start(x_scale[r:P:32, :].bitcast(I32), spread_scale[32 + 4 * r : 96 : 16, :].bitcast(I32))
-        memory.append(keep.tile([P, U], F32, name="memory1", tag="scales_then_memory"))
+        memory.append(shared.tile([P, U], F32, name="memory1", offset=0))
         nc.sync.dma_start(memory[1][:], mem[P : 2 * P, :])
+        new_row = shared.tile([P, S], F32, name="new_row", offset=block_bytes)
+        nc.sync.dma_start(new_row[:, HALF:S], new[:, HALF:S])
+        nc.sync.dma_start(new_row[:, 0:HALF], new[:, 0:HALF])
 
         def bank(number, name):
             return psum.tile([P, HALF], F32, name=name, tag=f"bank{number}")
@@ -97,11 +103,10 @@ def tile_picked_ema_none_p_kernel(
                     nc.tensor.transpose(wide[:, cols(c)], factors[:, column : column + 1].to_broadcast([P, P]), identity[:])
                 nc.scalar.copy(place, wide[:])
 
-        fresh = keep.tile([P, S], F32, name="old_then_fresh")
-        old_row = [fresh[:, first], fresh[:, second]]
-        new_row = keep.tile([P, S], F32, name="new_row")
+        line = keep.tile([P, 3 * HALF], F32, name="line")
+        old_row = [line[:, cols(0, HALF)], line[:, cols(2, HALF)]]
+        fresh = line[:, HALF : 3 * HALF]
         spread_row("old_row", OLD_ROW, old_row, 1)
-        spread_row("new_row", NEW_ROW, [new_row[:, first], new_row[:, second]], 3)
 
         kept = [keep.tile([P, S], F32, name=f"kept{b}") for b in range(ROW_BLOCKS)]
 
@@ -117,9 +122,9 @@ def tile_picked_ema_none_p_kernel(
         nc.scalar.copy(kept_turned[:], wide[:])
         look_up(0, 1)
 
-        pieces = (range(0, 2), range(2, 4), range(4, 8))
+        pieces = (range(0, 2), range(2, 4))
         back = [bank(5 + i, f"back{i}") for i in range(len(pieces))]
-        for chunks, sums in zip(pieces[:2], back):
+        for chunks, sums in zip(pieces, back):
             for i, c in enumerate(chunks):
                 nc.tensor.matmul(sums[:, cols(i)], kept_turned[:, cols(c)], identity[:], is_transpose=True, start=i == 0, stop=False)
 
@@ -145,8 +150,8 @@ def tile_picked_ema_none_p_kernel(
         def weights(b):
             return w_codes[:, cols(b)], w_scale[:, cols(b)]
 
-        scaled = keep.tile([P, S], F32, name="scaled")
-        blend = keep.tile([P, HALF], F32, name="blend")
+        scaled = keep.tile([P, HALF], F32, name="scaled")
+        blend = keep.tile([P, 3 * QUARTER], F32, name="blend")
 
         def project(chunks, number):
             product = bank(number, f"product{chunks[0]}")
@@ -162,31 +167,30 @@ def tile_picked_ema_none_p_kernel(
             nc.scalar.copy(blend[:, chunks[0] * P : (chunks[-1] + 1) * P], back[piece][:, 0 : len(chunks) * P])
 
         def put(quarter, sums):
-            nc.scalar.activation(memory[0][:].indirect(slots(cols(quarter, S // 4))), sums[:, cols(quarter % 2, S // 4)], COPY)
+            nc.scalar.activation(memory[0][:].indirect(slots(cols(quarter, QUARTER))), sums, COPY)
 
-        def scale_rows(h, number):
-            rows = bank(number, f"rows{h}")
-            multiply(rows[:], weights(1), picked(cols(h, HALF)))
+        def wide_product(b, h, number):
+            rows = bank(number, f"rows{b}_{h}")
+            multiply(rows[:], weights(b), picked(cols(h, HALF)))
             return rows
 
         project(pieces[0], 0)
         project(pieces[1], 1)
         turn_back(0)
-        put(0, blend)
-        project(pieces[2], 1)
         turn_back(1)
-        rows = [scale_rows(0, 5), scale_rows(1, 0)]
-        put(1, blend)
-        for i, c in enumerate(pieces[2]):
-            nc.tensor.transpose(back[2][:, cols(i)], scaled[:, cols(c)], identity[:])
+        put(0, blend[:, cols(0, QUARTER)])
+        put(1, blend[:, cols(1, QUARTER)])
 
-        for h in range(S // HALF):
-            look_up(1, h)
-        for h in range(S // HALF):
-            nc.vector.tensor_tensor(fresh[:, cols(h, HALF)], rows[h][:], new_row[:, cols(h, HALF)], MULT)
-        nc.vector.tensor_tensor(new_row[:, first], back[2][:], kept[0][:, second], ADD)
-        put(2, new_row[:, first])
-        put(3, new_row[:, first])
+        late = old_row[0]
+        look_up(1, 0)
+        nc.vector.tensor_tensor(late, wide_product(0, 1, 0)[:], new_row[:, second], MULT)
+        look_up(1, 1)
+        nc.vector.tensor_tensor(blend[:, cols(2, QUARTER)], late[:, cols(0, QUARTER)], kept[0][:, cols(2, QUARTER)], ADD)
+        put(2, blend[:, cols(2, QUARTER)])
+        nc.vector.tensor_tensor(fresh[:, first], wide_product(1, 0, 0)[:], new_row[:, first], MULT)
+        nc.vector.tensor_tensor(fresh[:, second], wide_product(1, 1, 1)[:], new_row[:, second], MULT)
+        nc.vector.tensor_tensor(new_row[:, cols(0, QUARTER)], late[:, cols(1, QUARTER)], kept[0][:, cols(3, QUARTER)], ADD)
+        put(3, new_row[:, cols(0, QUARTER)])
         nc.scalar.dma_start(out[0:P, :], memory[0][:])
-        nc.vector.tensor_tensor(memory[1][:].indirect(slot_sb[:]), kept[1][:], fresh[:], ADD)
+        nc.vector.tensor_tensor(memory[1][:].indirect(slot_sb[:]), kept[1][:], fresh, ADD)
         nc.sync.dma_start(out[P : 2 * P, :], memory[1][:])

@@ -33,22 +33,20 @@ def tile_picked_ema_none_p_kernel(
     nc = tc.nc
     with ExitStack() as ctx:
         keep = ctx.enter_context(tc.tile_pool(name="keep", bufs=1))
-        shared = ctx.enter_context(tc.tile_pool(name="shared", bufs=1))
         psum = ctx.enter_context(tc.psum_pool(name="psum", bufs=1))
 
         offs_sb = keep.tile([P, S // STRIPE], U16, name="offs_sb")
         slot_sb = keep.tile([P, S // STRIPE], U16, name="slot_sb")
         words = keep.tile([P, T], U32, name="words")
-        block_bytes = 4 * U
-        scales = shared.tile([P, T], U8, name="scales", offset=block_bytes - T // 2)
+        scales = keep.tile([P, T], U8, name="scales")
         memory = [keep.tile([P, U], F32, name="memory0")]
         w_raw = keep.tile([P, PACK, N], F32, name="w_raw")
         factor_rows = keep.tile([P, P], F32, name="factor_rows")
         identity = keep.tile([P, P], F32, name="identity")
         x_scale = keep.tile([P, S], U8, name="x_scale", align_bytes=64)
 
-        NEW_ROW = P - PER_HALF
-        OLD_ROW = NEW_ROW - CHUNKS
+        OLD_ROW = P - 2 * CHUNKS
+        NEW_ROW = P - CHUNKS
         nc.vector.memset(scales[:].bitcast(I32), 0)
         nc.vector.memset(x_scale[:].bitcast(I32), 0)
         nc.vector.memset(factor_rows[0:OLD_ROW, :], 0.0)
@@ -58,7 +56,7 @@ def tile_picked_ema_none_p_kernel(
         nc.sync.dma_start(w_raw[:], w1.rearrange("(p j) n -> p j n", j=PACK))
         nc.sync.dma_start(offs_sb[:], offs)
         nc.sync.dma_start(slot_sb[:], slot)
-        nc.scalar.dma_start(factor_rows[NEW_ROW:P, :], new[0:1, 0:HALF].rearrange("r (c i) -> (r c) i", i=P))
+        nc.scalar.dma_start(factor_rows[NEW_ROW:P, :], new[0:1, :].rearrange("r (c i) -> (r c) i", i=P))
         nc.sync.dma_start(scales[32:96:4, :].bitcast(I32), x_scales[0].bitcast(I32))
         nc.sync.dma_start(memory[0][:], mem[0:P, :])
         nc.sync.dma_start(words[:].bitcast(I32), x_words[0].rearrange("p n t -> p (n t)").bitcast(I32))
@@ -67,11 +65,6 @@ def tile_picked_ema_none_p_kernel(
         nc.vector.tensor_copy(spread_scale[:], scales[:].indirect(offs_sb[:]))
         for r in range(4):
             nc.sync.dma_start(x_scale[r:P:32, :].bitcast(I32), spread_scale[32 + 4 * r : 96 : 16, :].bitcast(I32))
-        memory.append(shared.tile([P, U], F32, name="memory1", offset=0))
-        nc.sync.dma_start(memory[1][:], mem[P : 2 * P, :])
-        new_row = shared.tile([P, S], F32, name="new_row", offset=block_bytes)
-        nc.sync.dma_start(new_row[:, HALF:S], new[:, HALF:S])
-        nc.sync.dma_start(new_row[:, 0:HALF], new[:, 0:HALF])
 
         def bank(number, name):
             return psum.tile([P, HALF], F32, name=name, tag=f"bank{number}")
@@ -96,37 +89,43 @@ def tile_picked_ema_none_p_kernel(
         nc.vector.quantize_mx(out=w_codes[:].bitcast(FP8X4), scales=w_scale[:], in_=w_grouped[:].rearrange("p n j -> p (n j)"))
 
         def spread_row(name, row, places, number):
-            for h, place in enumerate(places):
+            for h, copies in enumerate(places):
                 wide = bank(number + h, f"{name}{h}")
                 for c in range(PER_HALF):
                     column = row + h * PER_HALF + c
                     nc.tensor.transpose(wide[:, cols(c)], factors[:, column : column + 1].to_broadcast([P, P]), identity[:])
-                nc.scalar.copy(place, wide[:])
+                for place in copies:
+                    nc.scalar.copy(place, wide[:])
 
-        line = keep.tile([P, 3 * HALF], F32, name="line")
-        old_row = [line[:, cols(0, HALF)], line[:, cols(2, HALF)]]
-        fresh = line[:, HALF : 3 * HALF]
-        spread_row("old_row", OLD_ROW, old_row, 1)
+        fresh = keep.tile([P, S], F32, name="old_then_fresh")
+        old_row = [fresh[:, first], fresh[:, second]]
+        old_early = keep.tile([P, HALF], F32, name="old_early", tag="old_then_memory")
+        spread_row("old_row", OLD_ROW, [[old_row[0]], [old_early[:], old_row[1]]], 1)
 
         kept = [keep.tile([P, S], F32, name=f"kept{b}") for b in range(ROW_BLOCKS)]
 
-        def look_up(b, h):
+        def look_up(b, h, factor):
             entries = cols(h, HALF)
-            nc.vector.tensor_tensor(kept[b][:, entries], memory[b][:].indirect(slots(entries)), old_row[h], MULT)
+            nc.vector.tensor_tensor(kept[b][:, entries], memory[b][:].indirect(slots(entries)), factor, MULT)
 
-        kept_turned = keep.tile([P, HALF], F32, name="kept_turned")
-        look_up(0, 0)
+        kept_turned = keep.tile([P, HALF], F32, name="kept_turned", tag="turned_then_new")
+        look_up(0, 0, old_row[0])
         wide = bank(0, "kept_wide")
         for c in range(PER_HALF):
             nc.tensor.transpose(wide[:, cols(c)], kept[0][:, cols(c)], identity[:])
         nc.scalar.copy(kept_turned[:], wide[:])
-        look_up(0, 1)
+        look_up(0, 1, old_early[:])
+        memory.append(keep.tile([P, U], F32, name="memory1", tag="old_then_memory"))
+        nc.sync.dma_start(memory[1][:], mem[P : 2 * P, :])
 
         pieces = (range(0, 2), range(2, 4))
         back = [bank(5 + i, f"back{i}") for i in range(len(pieces))]
         for chunks, sums in zip(pieces, back):
             for i, c in enumerate(chunks):
                 nc.tensor.matmul(sums[:, cols(i)], kept_turned[:, cols(c)], identity[:], is_transpose=True, start=i == 0, stop=False)
+
+        new_row = keep.tile([P, S], F32, name="new_row", tag="turned_then_new")
+        nc.sync.dma_start(new_row[:], new)
 
         x_codes = keep.tile([P, S], U32, name="x_codes", align_bytes=64)
         for a, z in ((0, S // 4), (S // 4, HALF), (HALF, S)):
@@ -150,8 +149,8 @@ def tile_picked_ema_none_p_kernel(
         def weights(b):
             return w_codes[:, cols(b)], w_scale[:, cols(b)]
 
-        scaled = keep.tile([P, HALF], F32, name="scaled")
-        blend = keep.tile([P, 3 * QUARTER], F32, name="blend")
+        scaled = keep.tile([P, S], F32, name="scaled")
+        blend = keep.tile([P, HALF], F32, name="blend")
 
         def project(chunks, number):
             product = bank(number, f"product{chunks[0]}")
@@ -179,18 +178,20 @@ def tile_picked_ema_none_p_kernel(
         turn_back(0)
         turn_back(1)
         put(0, blend[:, cols(0, QUARTER)])
+        project(range(PER_HALF, CHUNKS), 1)
+        rows = [wide_product(1, 0, 5), wide_product(1, 1, 0)]
         put(1, blend[:, cols(1, QUARTER)])
+        late = bank(7, "late")
+        for i in range(PER_HALF):
+            nc.tensor.transpose(late[:, cols(i)], scaled[:, cols(PER_HALF + i)], identity[:])
 
-        late = old_row[0]
-        look_up(1, 0)
-        nc.vector.tensor_tensor(late, wide_product(0, 1, 0)[:], new_row[:, second], MULT)
-        look_up(1, 1)
-        nc.vector.tensor_tensor(blend[:, cols(2, QUARTER)], late[:, cols(0, QUARTER)], kept[0][:, cols(2, QUARTER)], ADD)
-        put(2, blend[:, cols(2, QUARTER)])
-        nc.vector.tensor_tensor(fresh[:, first], wide_product(1, 0, 0)[:], new_row[:, first], MULT)
-        nc.vector.tensor_tensor(fresh[:, second], wide_product(1, 1, 1)[:], new_row[:, second], MULT)
-        nc.vector.tensor_tensor(new_row[:, cols(0, QUARTER)], late[:, cols(1, QUARTER)], kept[0][:, cols(3, QUARTER)], ADD)
-        put(3, new_row[:, cols(0, QUARTER)])
+        for h in range(S // HALF):
+            look_up(1, h, old_row[h])
+        for h in range(S // HALF):
+            nc.vector.tensor_tensor(fresh[:, cols(h, HALF)], rows[h][:], new_row[:, cols(h, HALF)], MULT)
+        nc.vector.tensor_tensor(new_row[:, first], late[:], kept[0][:, second], ADD)
+        put(2, new_row[:, cols(0, QUARTER)])
+        put(3, new_row[:, cols(1, QUARTER)])
         nc.scalar.dma_start(out[0:P, :], memory[0][:])
-        nc.vector.tensor_tensor(memory[1][:].indirect(slot_sb[:]), kept[1][:], fresh, ADD)
+        nc.vector.tensor_tensor(memory[1][:].indirect(slot_sb[:]), kept[1][:], fresh[:], ADD)
         nc.sync.dma_start(out[P : 2 * P, :], memory[1][:])

@@ -97,10 +97,13 @@ def tile_picked_ema_none_p_kernel(
                 for place in copies:
                     nc.scalar.copy(place, wide[:])
 
-        fresh = keep.tile([P, S], F32, name="old_then_fresh")
-        old_row = [fresh[:, first], fresh[:, second]]
+        line = keep.tile([P, 3 * HALF], F32, name="line")
+        old_row = [line[:, cols(0, HALF)], line[:, cols(2, HALF)]]
+        fresh = line[:, HALF : 3 * HALF]
+        new_first = keep.tile([P, HALF], F32, name="new_first")
         old_early = keep.tile([P, HALF], F32, name="old_early", tag="old_then_memory")
         spread_row("old_row", OLD_ROW, [[old_row[0]], [old_early[:], old_row[1]]], 1)
+        spread_row("new_row", NEW_ROW, [[new_first[:]]], 3)
 
         kept = [keep.tile([P, S], F32, name=f"kept{b}") for b in range(ROW_BLOCKS)]
 
@@ -115,6 +118,11 @@ def tile_picked_ema_none_p_kernel(
             nc.tensor.transpose(wide[:, cols(c)], kept[0][:, cols(c)], identity[:])
         nc.scalar.copy(kept_turned[:], wide[:])
         look_up(0, 1, old_early[:])
+        last_turned = keep.tile([P, QUARTER], F32, name="last_turned")
+        wide = bank(4, "last_wide")
+        for i in range(2):
+            nc.tensor.transpose(wide[:, cols(i)], kept[0][:, cols(CHUNKS - 2 + i)], identity[:])
+        nc.scalar.copy(last_turned[:], wide[:, 0:QUARTER])
         memory.append(keep.tile([P, U], F32, name="memory1", tag="old_then_memory"))
         nc.sync.dma_start(memory[1][:], mem[P : 2 * P, :])
 
@@ -124,8 +132,8 @@ def tile_picked_ema_none_p_kernel(
             for i, c in enumerate(chunks):
                 nc.tensor.matmul(sums[:, cols(i)], kept_turned[:, cols(c)], identity[:], is_transpose=True, start=i == 0, stop=False)
 
-        new_row = keep.tile([P, S], F32, name="new_row", tag="turned_then_new")
-        nc.sync.dma_start(new_row[:], new)
+        new_second = keep.tile([P, HALF], F32, name="new_second", tag="turned_then_new")
+        nc.sync.dma_start(new_second[:], new[:, second])
 
         x_codes = keep.tile([P, S], U32, name="x_codes", align_bytes=64)
         for a, z in ((0, S // 4), (S // 4, HALF), (HALF, S)):
@@ -150,7 +158,7 @@ def tile_picked_ema_none_p_kernel(
             return w_codes[:, cols(b)], w_scale[:, cols(b)]
 
         scaled = keep.tile([P, S], F32, name="scaled")
-        blend = keep.tile([P, HALF], F32, name="blend")
+        blend = keep.tile([P, 3 * QUARTER], F32, name="blend")
 
         def project(chunks, number):
             product = bank(number, f"product{chunks[0]}")
@@ -175,23 +183,28 @@ def tile_picked_ema_none_p_kernel(
 
         project(pieces[0], 0)
         project(pieces[1], 1)
+        nc.vector.tensor_tensor(fresh[:, first], wide_product(1, 0, 3)[:], new_first[:], MULT)
         turn_back(0)
         turn_back(1)
         put(0, blend[:, cols(0, QUARTER)])
         project(range(PER_HALF, CHUNKS), 1)
-        rows = [wide_product(1, 0, 5), wide_product(1, 1, 0)]
+        rows = wide_product(1, 1, 0)
         put(1, blend[:, cols(1, QUARTER)])
         late = bank(7, "late")
-        for i in range(PER_HALF):
+        for i in range(2):
             nc.tensor.transpose(late[:, cols(i)], scaled[:, cols(PER_HALF + i)], identity[:])
+        last = bank(5, "last")
+        for i in range(2):
+            nc.tensor.matmul(last[:, cols(i)], last_turned[:, cols(i)], identity[:], is_transpose=True, start=True, stop=False)
+            nc.tensor.matmul(last[:, cols(i)], scaled[:, cols(CHUNKS - 2 + i)], identity[:], is_transpose=True, start=False, stop=True)
+        nc.scalar.copy(blend[:, cols(2, QUARTER)], last[:, 0:QUARTER])
 
-        for h in range(S // HALF):
-            look_up(1, h, old_row[h])
-        for h in range(S // HALF):
-            nc.vector.tensor_tensor(fresh[:, cols(h, HALF)], rows[h][:], new_row[:, cols(h, HALF)], MULT)
-        nc.vector.tensor_tensor(new_row[:, first], late[:], kept[0][:, second], ADD)
-        put(2, new_row[:, cols(0, QUARTER)])
-        put(3, new_row[:, cols(1, QUARTER)])
-        nc.scalar.dma_start(out[0:P, :], memory[0][:])
-        nc.vector.tensor_tensor(memory[1][:].indirect(slot_sb[:]), kept[1][:], fresh[:], ADD)
-        nc.sync.dma_start(out[P : 2 * P, :], memory[1][:])
+        look_up(1, 1, old_row[1])
+        look_up(1, 0, old_row[0])
+        nc.vector.tensor_tensor(fresh[:, second], rows[:], new_second[:], MULT)
+        nc.vector.tensor_tensor(old_row[0][:, 0:QUARTER], late[:, 0:QUARTER], kept[0][:, cols(2, QUARTER)], ADD)
+        put(2, old_row[0][:, 0:QUARTER])
+        put(3, blend[:, cols(2, QUARTER)])
+        nc.sync.dma_start(out[0:P, :], memory[0][:])
+        nc.vector.tensor_tensor(memory[1][:].indirect(slot_sb[:]), kept[1][:], fresh, ADD)
+        nc.scalar.dma_start(out[P : 2 * P, :], memory[1][:])

@@ -38,7 +38,7 @@ def tile_picked_ema_none_p_kernel(
         offs_sb = keep.tile([P, S // STRIPE], U16, name="offs_sb")
         slot_sb = keep.tile([P, S // STRIPE], U16, name="slot_sb")
         words = keep.tile([P, T], U32, name="words")
-        scales = keep.tile([P, T], U8, name="scales")
+        scales = keep.tile([P, T], U8, name="scales", tag="scales_then_codes", align_bytes=64)
         memory = [keep.tile([P, U], F32, name="memory0")]
         w_raw = keep.tile([P, PACK, N], F32, name="w_raw")
         factor_rows = keep.tile([P, P], F32, name="factor_rows")
@@ -83,7 +83,7 @@ def tile_picked_ema_none_p_kernel(
         nc.scalar.copy(factors[:], turned[:, 0:P])
 
         w_grouped = keep.tile([P, N, PACK], BF16, name="w_grouped", align_bytes=64)
-        w_codes = keep.tile([P, N], U32, name="w_codes", align_bytes=64)
+        w_codes = keep.tile([P, N], U32, name="w_codes", tag="scales_then_codes", align_bytes=64)
         w_scale = keep.tile([P, N], U8, name="w_scale", align_bytes=64)
         nc.scalar.copy(w_grouped[:], w_raw[:].rearrange("p j n -> p n j"))
         nc.vector.quantize_mx(out=w_codes[:].bitcast(FP8X4), scales=w_scale[:], in_=w_grouped[:].rearrange("p n j -> p (n j)"))
@@ -97,13 +97,10 @@ def tile_picked_ema_none_p_kernel(
                 for place in copies:
                     nc.scalar.copy(place, wide[:])
 
-        line = keep.tile([P, 3 * HALF], F32, name="line")
-        old_row = [line[:, cols(0, HALF)], line[:, cols(2, HALF)]]
-        fresh = line[:, HALF : 3 * HALF]
-        new_first = keep.tile([P, HALF], F32, name="new_first")
+        fresh = keep.tile([P, S], F32, name="old_then_fresh")
+        old_row = [fresh[:, first], fresh[:, second]]
         old_early = keep.tile([P, HALF], F32, name="old_early", tag="old_then_memory")
         spread_row("old_row", OLD_ROW, [[old_row[0]], [old_early[:], old_row[1]]], 1)
-        spread_row("new_row", NEW_ROW, [[new_first[:]]], 3)
 
         kept = [keep.tile([P, S], F32, name=f"kept{b}") for b in range(ROW_BLOCKS)]
 
@@ -132,11 +129,11 @@ def tile_picked_ema_none_p_kernel(
             for i, c in enumerate(chunks):
                 nc.tensor.matmul(sums[:, cols(i)], kept_turned[:, cols(c)], identity[:], is_transpose=True, start=i == 0, stop=False)
 
-        new_second = keep.tile([P, HALF], F32, name="new_second", tag="turned_then_new")
-        nc.sync.dma_start(new_second[:], new[:, second])
+        new_row = keep.tile([P, S], F32, name="new_row", tag="turned_then_new")
+        nc.sync.dma_start(new_row[:], new)
 
         x_codes = keep.tile([P, S], U32, name="x_codes", align_bytes=64)
-        for a, z in ((0, S // 4), (S // 4, HALF), (HALF, S)):
+        for a, z in ((0, QUARTER), (QUARTER, HALF), (HALF, S)):
             nc.vector.tensor_copy(x_codes[:, a:z], words[:].indirect(offs_sb[:, a // STRIPE : z // STRIPE]))
 
         def multiply(place, stationary, moving):
@@ -176,35 +173,32 @@ def tile_picked_ema_none_p_kernel(
         def put(quarter, sums):
             nc.scalar.activation(memory[0][:].indirect(slots(cols(quarter, QUARTER))), sums, COPY)
 
-        def wide_product(b, h, number):
-            rows = bank(number, f"rows{b}_{h}")
-            multiply(rows[:], weights(b), picked(cols(h, HALF)))
-            return rows
-
         project(pieces[0], 0)
         project(pieces[1], 1)
-        nc.vector.tensor_tensor(fresh[:, first], wide_product(1, 0, 3)[:], new_first[:], MULT)
         turn_back(0)
         turn_back(1)
         put(0, blend[:, cols(0, QUARTER)])
         project(range(PER_HALF, CHUNKS), 1)
-        rows = wide_product(1, 1, 0)
+        rows = [bank(5 + h, f"rows{h}") for h in range(S // HALF)]
+        for h in range(S // HALF):
+            multiply(rows[h][:], weights(1), picked(cols(h, HALF)))
         put(1, blend[:, cols(1, QUARTER)])
         late = bank(7, "late")
         for i in range(2):
             nc.tensor.transpose(late[:, cols(i)], scaled[:, cols(PER_HALF + i)], identity[:])
-        last = bank(5, "last")
+        last = bank(3, "last")
         for i in range(2):
             nc.tensor.matmul(last[:, cols(i)], last_turned[:, cols(i)], identity[:], is_transpose=True, start=True, stop=False)
             nc.tensor.matmul(last[:, cols(i)], scaled[:, cols(CHUNKS - 2 + i)], identity[:], is_transpose=True, start=False, stop=True)
         nc.scalar.copy(blend[:, cols(2, QUARTER)], last[:, 0:QUARTER])
 
-        look_up(1, 1, old_row[1])
-        look_up(1, 0, old_row[0])
-        nc.vector.tensor_tensor(fresh[:, second], rows[:], new_second[:], MULT)
-        nc.vector.tensor_tensor(old_row[0][:, 0:QUARTER], late[:, 0:QUARTER], kept[0][:, cols(2, QUARTER)], ADD)
-        put(2, old_row[0][:, 0:QUARTER])
+        for h in range(S // HALF):
+            look_up(1, h, old_row[h])
+        for h in range(S // HALF):
+            nc.vector.tensor_tensor(fresh[:, cols(h, HALF)], rows[h][:], new_row[:, cols(h, HALF)], MULT)
+        nc.vector.tensor_tensor(new_row[:, 0:QUARTER], late[:, 0:QUARTER], kept[0][:, cols(2, QUARTER)], ADD)
+        put(2, new_row[:, 0:QUARTER])
         put(3, blend[:, cols(2, QUARTER)])
         nc.sync.dma_start(out[0:P, :], memory[0][:])
-        nc.vector.tensor_tensor(memory[1][:].indirect(slot_sb[:]), kept[1][:], fresh, ADD)
+        nc.vector.tensor_tensor(memory[1][:].indirect(slot_sb[:]), kept[1][:], fresh[:], ADD)
         nc.scalar.dma_start(out[P : 2 * P, :], memory[1][:])

@@ -52,7 +52,7 @@ def tile_picked_ema_none_p_kernel(
         nc.vector.memset(factor_rows[0:OLD_ROW, :], 0.0)
         make_identity(nc, identity[:])
 
-        nc.sync.dma_start(factor_rows[OLD_ROW:NEW_ROW, :], old[0:1, :].rearrange("r (c i) -> (r c) i", i=P))
+        nc.scalar.dma_start(factor_rows[OLD_ROW:NEW_ROW, :], old[0:1, :].rearrange("r (c i) -> (r c) i", i=P))
         nc.sync.dma_start(w_raw[:], w1.rearrange("(p j) n -> p j n", j=PACK))
         nc.sync.dma_start(offs_sb[:], offs)
         nc.sync.dma_start(slot_sb[:], slot)
@@ -201,4 +201,4 @@ def tile_picked_ema_none_p_kernel(
         put(3, blend[:, cols(2, QUARTER)])
         nc.sync.dma_start(out[0:P, :], memory[0][:])
         nc.vector.tensor_tensor(memory[1][:].indirect(slot_sb[:]), kept[1][:], fresh[:], ADD)
-        nc.scalar.dma_start(out[P : 2 * P, :], memory[1][:])
+        nc.sync.dma_start(out[P : 2 * P, :], memory[1][:])

@@ -100,7 +100,7 @@ def tile_picked_ema_none_p_kernel(
         fresh = keep.tile([P, S], F32, name="old_then_fresh")
         old_row = [fresh[:, first], fresh[:, second]]
         old_early = keep.tile([P, HALF], F32, name="old_early", tag="old_then_memory")
-        spread_row("old_row", OLD_ROW, [[old_row[0]], [old_early[:], old_row[1]]], 1)
+        spread_row("old_row", OLD_ROW, [[old_early[:], old_row[0]], [old_row[1]]], 1)
 
         kept = [keep.tile([P, S], F32, name=f"kept{b}") for b in range(ROW_BLOCKS)]
 
@@ -109,12 +109,12 @@ def tile_picked_ema_none_p_kernel(
             nc.vector.tensor_tensor(kept[b][:, entries], memory[b][:].indirect(slots(entries)), factor, MULT)
 
         kept_turned = keep.tile([P, HALF], F32, name="kept_turned", tag="turned_then_new")
-        look_up(0, 0, old_row[0])
+        look_up(0, 0, old_early[:])
         wide = bank(0, "kept_wide")
         for c in range(PER_HALF):
             nc.tensor.transpose(wide[:, cols(c)], kept[0][:, cols(c)], identity[:])
         nc.scalar.copy(kept_turned[:], wide[:])
-        look_up(0, 1, old_early[:])
+        look_up(0, 1, old_row[1])
         last_turned = keep.tile([P, QUARTER], F32, name="last_turned")
         wide = bank(4, "last_wide")
         for i in range(2):

@@ -157,8 +157,7 @@ def tile_picked_ema_none_p_kernel(
         scaled = keep.tile([P, S], F32, name="scaled")
         blend = keep.tile([P, 3 * QUARTER], F32, name="blend")
 
-        def project(chunks, number):
-            product = bank(number, f"product{chunks[0]}")
+        def project(chunks, product):
             for i, c in enumerate(chunks):
                 multiply(product[:, cols(i)], picked(cols(c)), weights(0))
             for i, c in enumerate(chunks):
@@ -173,19 +172,20 @@ def tile_picked_ema_none_p_kernel(
         def put(quarter, sums):
             nc.scalar.activation(memory[0][:].indirect(slots(cols(quarter, QUARTER))), sums, COPY)
 
-        project(pieces[0], 0)
-        project(pieces[1], 1)
+        project(pieces[0], bank(0, "product0"))
+        for c in pieces[1]:
+            project(range(c, c + 1), bank(c - 1, f"product{c}"))
         turn_back(0)
         turn_back(1)
         put(0, blend[:, cols(0, QUARTER)])
-        project(range(PER_HALF, CHUNKS), 1)
+        third = cols(2, QUARTER)
+        project(range(CHUNKS - 2, CHUNKS), bank(2, "last_products"))
+        late = bank(1, "late")[:, 0:QUARTER]
+        multiply(late, weights(0), picked(third))
         rows = [bank(5 + h, f"rows{h}") for h in range(S // HALF)]
         for h in range(S // HALF):
             multiply(rows[h][:], weights(1), picked(cols(h, HALF)))
         put(1, blend[:, cols(1, QUARTER)])
-        late = bank(7, "late")
-        for i in range(2):
-            nc.tensor.transpose(late[:, cols(i)], scaled[:, cols(PER_HALF + i)], identity[:])
         last = bank(3, "last")
         for i in range(2):
             nc.tensor.matmul(last[:, cols(i)], last_turned[:, cols(i)], identity[:], is_transpose=True, start=True, stop=False)
@@ -194,9 +194,11 @@ def tile_picked_ema_none_p_kernel(
 
         for h in range(S // HALF):
             look_up(1, h, old_row[h])
+        late_scaled = keep.tile([P, QUARTER], F32, name="late_scaled")
+        nc.vector.tensor_tensor(late_scaled[:], late, new_row[:, third], MULT)
         for h in range(S // HALF):
             nc.vector.tensor_tensor(fresh[:, cols(h, HALF)], rows[h][:], new_row[:, cols(h, HALF)], MULT)
-        nc.vector.tensor_tensor(new_row[:, 0:QUARTER], late[:, 0:QUARTER], kept[0][:, cols(2, QUARTER)], ADD)
+        nc.vector.tensor_tensor(new_row[:, 0:QUARTER], late_scaled[:], kept[0][:, third], ADD)
         put(2, new_row[:, 0:QUARTER])
         put(3, blend[:, cols(2, QUARTER)])
         nc.sync.dma_start(out[0:P, :], memory[0][:])

@@ -52,8 +52,8 @@ def tile_picked_ema_none_p_kernel(
         nc.vector.memset(factor_rows[0:OLD_ROW, :], 0.0)
         make_identity(nc, identity[:])
 
-        nc.scalar.dma_start(factor_rows[OLD_ROW:NEW_ROW, :], old[0:1, :].rearrange("r (c i) -> (r c) i", i=P))
-        nc.sync.dma_start(w_raw[:], w1.rearrange("(p j) n -> p j n", j=PACK))
+        nc.scalar.dma_start(w_raw[:], w1.rearrange("(p j) n -> p j n", j=PACK))
+        nc.sync.dma_start(factor_rows[OLD_ROW:NEW_ROW, :], old[0:1, :].rearrange("r (c i) -> (r c) i", i=P))
         nc.sync.dma_start(offs_sb[:], offs)
         nc.sync.dma_start(slot_sb[:], slot)
         nc.scalar.dma_start(factor_rows[NEW_ROW:P, :], new[0:1, :].rearrange("r (c i) -> (r c) i", i=P))

@@ -43,12 +43,10 @@ def tile_picked_ema_none_p_kernel(
         w_raw = keep.tile([P, PACK, N], F32, name="w_raw")
         factor_rows = keep.tile([P, P], F32, name="factor_rows")
         identity = keep.tile([P, P], F32, name="identity")
-        x_scale = keep.tile([P, S], U8, name="x_scale", align_bytes=64)
 
         OLD_ROW = P - 2 * CHUNKS
         NEW_ROW = P - CHUNKS
         nc.vector.memset(scales[:].bitcast(I32), 0)
-        nc.vector.memset(x_scale[:].bitcast(I32), 0)
         nc.vector.memset(factor_rows[0:OLD_ROW, :], 0.0)
         make_identity(nc, identity[:])
 
@@ -63,8 +61,6 @@ def tile_picked_ema_none_p_kernel(
 
         spread_scale = keep.tile([P, S], U8, name="spread_scale")
         nc.vector.tensor_copy(spread_scale[:], scales[:].indirect(offs_sb[:]))
-        for r in range(4):
-            nc.sync.dma_start(x_scale[r:P:32, :].bitcast(I32), spread_scale[32 + 4 * r : 96 : 16, :].bitcast(I32))
 
         def bank(number, name):
             return psum.tile([P, HALF], F32, name=name, tag=f"bank{number}")
@@ -77,10 +73,12 @@ def tile_picked_ema_none_p_kernel(
 
         first, second = cols(0, HALF), cols(1, HALF)
 
-        factors = keep.tile([P, P], F32, name="factors")
+        old_factors = keep.tile([P, CHUNKS], F32, name="old_factors", tag="old_then_scales", align_bytes=64)
+        new_factors = keep.tile([P, CHUNKS], F32, name="new_factors")
         turned = bank(0, "turned_factors")
         nc.tensor.transpose(turned[:, 0:P], factor_rows[:], identity[:])
-        nc.scalar.copy(factors[:], turned[:, 0:P])
+        nc.scalar.copy(old_factors[:], turned[:, OLD_ROW:NEW_ROW])
+        nc.scalar.copy(new_factors[:], turned[:, NEW_ROW:P])
 
         w_grouped = keep.tile([P, N, PACK], BF16, name="w_grouped", align_bytes=64)
         w_codes = keep.tile([P, N], U32, name="w_codes", tag="scales_then_codes", align_bytes=64)
@@ -88,19 +86,24 @@ def tile_picked_ema_none_p_kernel(
         nc.scalar.copy(w_grouped[:], w_raw[:].rearrange("p j n -> p n j"))
         nc.vector.quantize_mx(out=w_codes[:].bitcast(FP8X4), scales=w_scale[:], in_=w_grouped[:].rearrange("p n j -> p (n j)"))
 
-        def spread_row(name, row, places, number):
+        def spread_row(name, places, number):
             for h, copies in enumerate(places):
                 wide = bank(number + h, f"{name}{h}")
                 for c in range(PER_HALF):
-                    column = row + h * PER_HALF + c
-                    nc.tensor.transpose(wide[:, cols(c)], factors[:, column : column + 1].to_broadcast([P, P]), identity[:])
+                    column = h * PER_HALF + c
+                    nc.tensor.transpose(wide[:, cols(c)], old_factors[:, column : column + 1].to_broadcast([P, P]), identity[:])
                 for place in copies:
                     nc.scalar.copy(place, wide[:])
 
         fresh = keep.tile([P, S], F32, name="old_then_fresh")
         old_row = [fresh[:, first], fresh[:, second]]
         old_early = keep.tile([P, HALF], F32, name="old_early", tag="old_then_memory")
-        spread_row("old_row", OLD_ROW, [[old_early[:], old_row[0]], [old_row[1]]], 1)
+        spread_row("old_row", [[old_early[:], old_row[0]], [old_row[1]]], 1)
+
+        x_scale = keep.tile([P, S], U8, name="x_scale", tag="old_then_scales", align_bytes=64)
+        nc.gpsimd.memset(x_scale[:].bitcast(I32), 0)
+        for r in range(4):
+            nc.scalar.dma_start(x_scale[r:P:32, :].bitcast(I32), spread_scale[32 + 4 * r : 96 : 16, :].bitcast(I32))
 
         kept = [keep.tile([P, S], F32, name=f"kept{b}") for b in range(ROW_BLOCKS)]
 
@@ -161,7 +164,7 @@ def tile_picked_ema_none_p_kernel(
             for i, c in enumerate(chunks):
                 multiply(product[:, cols(i)], picked(cols(c)), weights(0))
             for i, c in enumerate(chunks):
-                nc.scalar.activation(scaled[:, cols(c)], product[:, cols(i)], COPY, scale=factors[:, NEW_ROW + c : NEW_ROW + c + 1])
+                nc.scalar.activation(scaled[:, cols(c)], product[:, cols(i)], COPY, scale=new_factors[:, c : c + 1])
 
         def turn_back(piece):
             chunks = pieces[piece]

@@ -52,9 +52,9 @@ def tile_picked_ema_none_p_kernel(
 
         nc.scalar.dma_start(w_raw[:], w1.rearrange("(p j) n -> p j n", j=PACK))
         nc.sync.dma_start(factor_rows[OLD_ROW:NEW_ROW, :], old[0:1, :].rearrange("r (c i) -> (r c) i", i=P))
+        nc.sync.dma_start(factor_rows[NEW_ROW:P, :], new[0:1, :].rearrange("r (c i) -> (r c) i", i=P))
         nc.sync.dma_start(offs_sb[:], offs)
         nc.sync.dma_start(slot_sb[:], slot)
-        nc.scalar.dma_start(factor_rows[NEW_ROW:P, :], new[0:1, :].rearrange("r (c i) -> (r c) i", i=P))
         nc.sync.dma_start(scales[32:96:4, :].bitcast(I32), x_scales[0].bitcast(I32))
         nc.sync.dma_start(memory[0][:], mem[0:P, :])
         nc.sync.dma_start(words[:].bitcast(I32), x_words[0].rearrange("p n t -> p (n t)").bitcast(I32))
@@ -92,13 +92,13 @@ def tile_picked_ema_none_p_kernel(
                 for c in range(PER_HALF):
                     column = h * PER_HALF + c
                     nc.tensor.transpose(wide[:, cols(c)], old_factors[:, column : column + 1].to_broadcast([P, P]), identity[:])
-                for place in copies:
-                    nc.scalar.copy(place, wide[:])
+                for place, width in copies:
+                    nc.scalar.copy(place, wide[:, 0:width])
 
         fresh = keep.tile([P, S], F32, name="old_then_fresh")
         old_row = [fresh[:, first], fresh[:, second]]
-        old_early = keep.tile([P, HALF], F32, name="old_early", tag="old_then_memory")
-        spread_row("old_row", [[old_early[:], old_row[0]], [old_row[1]]], 1)
+        old_early = keep.tile([P, QUARTER], F32, name="old_early", tag="old_then_memory")
+        spread_row("old_row", [[(old_early[:], QUARTER), (old_row[0], HALF)], [(old_row[1], HALF)]], 1)
 
         x_scale = keep.tile([P, S], U8, name="x_scale", tag="old_then_scales", align_bytes=64)
         nc.gpsimd.memset(x_scale[:].bitcast(I32), 0)
@@ -107,17 +107,17 @@ def tile_picked_ema_none_p_kernel(
 
         kept = [keep.tile([P, S], F32, name=f"kept{b}") for b in range(ROW_BLOCKS)]
 
-        def look_up(b, h, factor):
-            entries = cols(h, HALF)
+        def look_up(b, entries, factor):
             nc.vector.tensor_tensor(kept[b][:, entries], memory[b][:].indirect(slots(entries)), factor, MULT)
 
         kept_turned = keep.tile([P, HALF], F32, name="kept_turned", tag="turned_then_new")
-        look_up(0, 0, old_early[:])
+        look_up(0, cols(0, QUARTER), old_early[:])
+        look_up(0, cols(1, QUARTER), fresh[:, cols(1, QUARTER)])
         wide = bank(0, "kept_wide")
         for c in range(PER_HALF):
             nc.tensor.transpose(wide[:, cols(c)], kept[0][:, cols(c)], identity[:])
         nc.scalar.copy(kept_turned[:], wide[:])
-        look_up(0, 1, old_row[1])
+        look_up(0, second, old_row[1])
         last_turned = keep.tile([P, QUARTER], F32, name="last_turned")
         wide = bank(4, "last_wide")
         for i in range(2):
@@ -196,7 +196,7 @@ def tile_picked_ema_none_p_kernel(
         nc.scalar.copy(blend[:, cols(2, QUARTER)], last[:, 0:QUARTER])
 
         for h in range(S // HALF):
-            look_up(1, h, old_row[h])
+            look_up(1, cols(h, HALF), old_row[h])
         late_scaled = keep.tile([P, QUARTER], F32, name="late_scaled")
         nc.vector.tensor_tensor(late_scaled[:], late, new_row[:, third], MULT)
         for h in range(S // HALF):

@@ -48,7 +48,8 @@ def tile_picked_ema_none_p_kernel(
         NEW_ROW = P - CHUNKS
         nc.vector.memset(scales[:].bitcast(I32), 0)
         nc.vector.memset(factor_rows[0:OLD_ROW, :], 0.0)
-        make_identity(nc, identity[:])
+        nc.vector.memset(identity[:], 0.0)
+        make_identity(nc, identity[:], nomemset=True)
 
         nc.scalar.dma_start(w_raw[:], w1.rearrange("(p j) n -> p j n", j=PACK))
         nc.sync.dma_start(factor_rows[OLD_ROW:NEW_ROW, :], old[0:1, :].rearrange("r (c i) -> (r c) i", i=P))
@@ -95,8 +96,9 @@ def tile_picked_ema_none_p_kernel(
                 for place, width in copies:
                     nc.scalar.copy(place, wide[:, 0:width])
 
-        fresh = keep.tile([P, S], F32, name="old_then_fresh")
-        old_row = [fresh[:, first], fresh[:, second]]
+        old_whole = keep.tile([P, S], F32, name="old_whole")
+        fresh = keep.tile([P, S], F32, name="fresh")
+        old_row = [old_whole[:, first], old_whole[:, second]]
         old_early = keep.tile([P, QUARTER], F32, name="old_early", tag="old_then_memory")
         spread_row("old_row", [[(old_early[:], QUARTER), (old_row[0], HALF)], [(old_row[1], HALF)]], 1)
 
@@ -112,7 +114,7 @@ def tile_picked_ema_none_p_kernel(
 
         kept_turned = keep.tile([P, HALF], F32, name="kept_turned", tag="turned_then_new")
         look_up(0, cols(0, QUARTER), old_early[:])
-        look_up(0, cols(1, QUARTER), fresh[:, cols(1, QUARTER)])
+        look_up(0, cols(1, QUARTER), old_whole[:, cols(1, QUARTER)])
         wide = bank(0, "kept_wide")
         for c in range(PER_HALF):
             nc.tensor.transpose(wide[:, cols(c)], kept[0][:, cols(c)], identity[:])
@@ -195,8 +197,7 @@ def tile_picked_ema_none_p_kernel(
             nc.tensor.matmul(last[:, cols(i)], scaled[:, cols(CHUNKS - 2 + i)], identity[:], is_transpose=True, start=False, stop=True)
         nc.scalar.copy(blend[:, cols(2, QUARTER)], last[:, 0:QUARTER])
 
-        for h in range(S // HALF):
-            look_up(1, cols(h, HALF), old_row[h])
+        look_up(1, slice(0, S), old_whole[:])
         late_scaled = keep.tile([P, QUARTER], F32, name="late_scaled")
         nc.vector.tensor_tensor(late_scaled[:], late, new_row[:, third], MULT)
         for h in range(S // HALF):

from contextlib import ExitStack

import concourse.mybir as mybir
from concourse.masks import make_identity

K, T, S, N, U = 512, 4096, 1024, 256, 2048
FLOPS = 2 * K * N * S

F32 = mybir.dt.float32
BF16 = mybir.dt.bfloat16
I32 = mybir.dt.int32
U32 = mybir.dt.uint32
U16 = mybir.dt.uint16
U8 = mybir.dt.uint8
FP8X4 = mybir.dt.float8_e4m3fn_x4
COPY = mybir.ActivationFunctionType.Copy
MULT = mybir.AluOpType.mult
ADD = mybir.AluOpType.add

P = 128
PACK = 4
STRIPE = 16
HALF = 512
CHUNKS = S // P
PER_HALF = HALF // P
ROW_BLOCKS = N // P
QUARTER = S // 4


def tile_picked_ema_none_p_kernel(
    tc, x_words, x_scales, mem, w1, old, new, offs, slot, out
):
    nc = tc.nc
    with ExitStack() as ctx:
        keep = ctx.enter_context(tc.tile_pool(name="keep", bufs=1))
        psum = ctx.enter_context(tc.psum_pool(name="psum", bufs=1))

        offs_sb = keep.tile([P, S // STRIPE], U16, name="offs_sb")
        slot_sb = keep.tile([P, S // STRIPE], U16, name="slot_sb")
        words = keep.tile([P, T], U32, name="words")
        scales = keep.tile([P, T], U8, name="scales", tag="scales_then_codes", align_bytes=64)
        memory = [keep.tile([P, U], F32, name="memory0")]
        w_raw = keep.tile([P, PACK, N], F32, name="w_raw")
        factor_rows = keep.tile([P, P], F32, name="factor_rows")
        identity = keep.tile([P, P], F32, name="identity")

        OLD_ROW = P - 2 * CHUNKS
        NEW_ROW = P - CHUNKS
        nc.vector.memset(scales[:].bitcast(I32), 0)
        nc.vector.memset(factor_rows[0:OLD_ROW, :], 0.0)
        nc.vector.memset(identity[:], 0.0)
        make_identity(nc, identity[:], nomemset=True)

        nc.scalar.dma_start(w_raw[:], w1.rearrange("(p j) n -> p j n", j=PACK))
        nc.sync.dma_start(factor_rows[OLD_ROW:NEW_ROW, :], old[0:1, :].rearrange("r (c i) -> (r c) i", i=P))
        nc.sync.dma_start(factor_rows[NEW_ROW:P, :], new[0:1, :].rearrange("r (c i) -> (r c) i", i=P))
        nc.sync.dma_start(offs_sb[:], offs)
        nc.sync.dma_start(slot_sb[:], slot)
        nc.sync.dma_start(scales[32:96:4, :].bitcast(I32), x_scales[0].bitcast(I32))
        nc.sync.dma_start(memory[0][:], mem[0:P, :])
        nc.sync.dma_start(words[:].bitcast(I32), x_words[0].rearrange("p n t -> p (n t)").bitcast(I32))

        spread_scale = keep.tile([P, S], U8, name="spread_scale")
        nc.vector.tensor_copy(spread_scale[:], scales[:].indirect(offs_sb[:]))

        def bank(number, name):
            return psum.tile([P, HALF], F32, name=name, tag=f"bank{number}")

        def cols(i, width=P):
            return slice(i * width, (i + 1) * width)

        def slots(entries):
            return slot_sb[:, entries.start // STRIPE : entries.stop // STRIPE]

        first, second = cols(0, HALF), cols(1, HALF)

        old_factors = keep.tile([P, CHUNKS], F32, name="old_factors", tag="old_then_scales", align_bytes=64)
        new_factors = keep.tile([P, CHUNKS], F32, name="new_factors")
        turned = bank(0, "turned_factors")
        nc.tensor.transpose(turned[:, 0:P], factor_rows[:], identity[:])
        nc.scalar.copy(old_factors[:], turned[:, OLD_ROW:NEW_ROW])
        nc.scalar.copy(new_factors[:], turned[:, NEW_ROW:P])

        w_grouped = keep.tile([P, N, PACK], BF16, name="w_grouped", align_bytes=64)
        w_codes = keep.tile([P, N], U32, name="w_codes", tag="scales_then_codes", align_bytes=64)
        w_scale = keep.tile([P, N], U8, name="w_scale", align_bytes=64)
        nc.scalar.copy(w_grouped[:], w_raw[:].rearrange("p j n -> p n j"))
        nc.vector.quantize_mx(out=w_codes[:].bitcast(FP8X4), scales=w_scale[:], in_=w_grouped[:].rearrange("p n j -> p (n j)"))

        def spread_row(name, places, number):
            for h, copies in enumerate(places):
                wide = bank(number + h, f"{name}{h}")
                for c in range(PER_HALF):
                    column = h * PER_HALF + c
                    nc.tensor.transpose(wide[:, cols(c)], old_factors[:, column : column + 1].to_broadcast([P, P]), identity[:])
                for place, width in copies:
                    nc.scalar.copy(place, wide[:, 0:width])

        old_whole = keep.tile([P, S], F32, name="old_whole")
        fresh = keep.tile([P, S], F32, name="fresh")
        old_row = [old_whole[:, first], old_whole[:, second]]
        old_early = keep.tile([P, QUARTER], F32, name="old_early", tag="old_then_memory")
        spread_row("old_row", [[(old_early[:], QUARTER), (old_row[0], HALF)], [(old_row[1], HALF)]], 1)

        x_scale = keep.tile([P, S], U8, name="x_scale", tag="old_then_scales", align_bytes=64)
        nc.gpsimd.memset(x_scale[:].bitcast(I32), 0)
        for r in range(4):
            nc.scalar.dma_start(x_scale[r:P:32, :].bitcast(I32), spread_scale[32 + 4 * r : 96 : 16, :].bitcast(I32))

        kept = [keep.tile([P, S], F32, name=f"kept{b}") for b in range(ROW_BLOCKS)]

        def look_up(b, entries, factor):
            nc.vector.tensor_tensor(kept[b][:, entries], memory[b][:].indirect(slots(entries)), factor, MULT)

        kept_turned = keep.tile([P, HALF], F32, name="kept_turned", tag="turned_then_new")
        look_up(0, cols(0, QUARTER), old_early[:])
        look_up(0, cols(1, QUARTER), old_whole[:, cols(1, QUARTER)])
        wide = bank(0, "kept_wide")
        for c in range(PER_HALF):
            nc.tensor.transpose(wide[:, cols(c)], kept[0][:, cols(c)], identity[:])
        nc.scalar.copy(kept_turned[:], wide[:])
        look_up(0, second, old_row[1])
        last_turned = keep.tile([P, QUARTER], F32, name="last_turned")
        wide = bank(4, "last_wide")
        for i in range(2):
            nc.tensor.transpose(wide[:, cols(i)], kept[0][:, cols(CHUNKS - 2 + i)], identity[:])
        nc.scalar.copy(last_turned[:], wide[:, 0:QUARTER])
        memory.append(keep.tile([P, U], F32, name="memory1", tag="old_then_memory"))
        nc.sync.dma_start(memory[1][:], mem[P : 2 * P, :])

        pieces = (range(0, 2), range(2, 4))
        back = [bank(5 + i, f"back{i}") for i in range(len(pieces))]
        for chunks, sums in zip(pieces, back):
            for i, c in enumerate(chunks):
                nc.tensor.matmul(sums[:, cols(i)], kept_turned[:, cols(c)], identity[:], is_transpose=True, start=i == 0, stop=False)

        new_row = keep.tile([P, S], F32, name="new_row", tag="turned_then_new")
        nc.sync.dma_start(new_row[:], new)

        x_codes = keep.tile([P, S], U32, name="x_codes", align_bytes=64)
        for a, z in ((0, QUARTER), (QUARTER, HALF), (HALF, S)):
            nc.vector.tensor_copy(x_codes[:, a:z], words[:].indirect(offs_sb[:, a // STRIPE : z // STRIPE]))

        def multiply(place, stationary, moving):
            (a_codes, a_scale), (b_codes, b_scale) = stationary, moving
            nc.tensor.matmul_mx(
                out=place,
                lhsT=a_codes.bitcast(FP8X4),
                lhsT_scale=a_scale,
                rhs=b_codes.bitcast(FP8X4),
                rhs_scale=b_scale,
                start=True,
                stop=True,
            )

        def picked(entries):
            return x_codes[:, entries], x_scale[:, entries]

        def weights(b):
            return w_codes[:, cols(b)], w_scale[:, cols(b)]

        scaled = keep.tile([P, S], F32, name="scaled")
        blend = keep.tile([P, 3 * QUARTER], F32, name="blend")

        def project(chunks, product):
            for i, c in enumerate(chunks):
                multiply(product[:, cols(i)], picked(cols(c)), weights(0))
            for i, c in enumerate(chunks):
                nc.scalar.activation(scaled[:, cols(c)], product[:, cols(i)], COPY, scale=new_factors[:, c : c + 1])

        def turn_back(piece):
            chunks = pieces[piece]
            for i, c in enumerate(chunks):
                nc.tensor.matmul(back[piece][:, cols(i)], scaled[:, cols(c)], identity[:], is_transpose=True, start=False, stop=c == chunks[-1])
            nc.scalar.copy(blend[:, chunks[0] * P : (chunks[-1] + 1) * P], back[piece][:, 0 : len(chunks) * P])

        def put(quarter, sums):
            nc.scalar.activation(memory[0][:].indirect(slots(cols(quarter, QUARTER))), sums, COPY)

        project(pieces[0], bank(0, "product0"))
        for c in pieces[1]:
            project(range(c, c + 1), bank(c - 1, f"product{c}"))
        turn_back(0)
        turn_back(1)
        put(0, blend[:, cols(0, QUARTER)])
        third = cols(2, QUARTER)
        project(range(CHUNKS - 2, CHUNKS), bank(2, "last_products"))
        late = bank(1, "late")[:, 0:QUARTER]
        multiply(late, weights(0), picked(third))
        rows = [bank(5 + h, f"rows{h}") for h in range(S // HALF)]
        for h in range(S // HALF):
            multiply(rows[h][:], weights(1), picked(cols(h, HALF)))
        put(1, blend[:, cols(1, QUARTER)])
        last = bank(3, "last")
        for i in range(2):
            nc.tensor.matmul(last[:, cols(i)], last_turned[:, cols(i)], identity[:], is_transpose=True, start=True, stop=False)
            nc.tensor.matmul(last[:, cols(i)], scaled[:, cols(CHUNKS - 2 + i)], identity[:], is_transpose=True, start=False, stop=True)
        nc.scalar.copy(blend[:, cols(2, QUARTER)], last[:, 0:QUARTER])

        look_up(1, slice(0, S), old_whole[:])
        late_scaled = keep.tile([P, QUARTER], F32, name="late_scaled")
        nc.vector.tensor_tensor(late_scaled[:], late, new_row[:, third], MULT)
        for h in range(S // HALF):
            nc.vector.tensor_tensor(fresh[:, cols(h, HALF)], rows[h][:], new_row[:, cols(h, HALF)], MULT)
        nc.vector.tensor_tensor(new_row[:, 0:QUARTER], late_scaled[:], kept[0][:, third], ADD)
        put(2, new_row[:, 0:QUARTER])
        put(3, blend[:, cols(2, QUARTER)])
        nc.sync.dma_start(out[0:P, :], memory[0][:])
        nc.vector.tensor_tensor(memory[1][:].indirect(slot_sb[:]), kept[1][:], fresh[:], ADD)
        nc.sync.dma_start(out[P : 2 * P, :], memory[1][:])
